import numpy as np
import ml_dtypes


def mxq(x, axis, fmt="e4m3"):
    dtype, down = {"e4m3": (ml_dtypes.float8_e4m3fn, 7), "e5m2": (ml_dtypes.float8_e5m2, 14)}[fmt]
    v = np.moveaxis(np.asarray(x, np.float32).astype(ml_dtypes.bfloat16).astype(np.float64), axis, -1)
    blocks = v.reshape(v.shape[:-1] + (-1, 32))
    amax = np.abs(blocks).max(-1, keepdims=True)
    byte = np.maximum(np.where(amax > 0, np.frexp(amax)[1] - 1 + 127, 0) - down, 1)
    scale = np.exp2(byte - 127.0)
    codes = (blocks / scale).astype(np.float32).astype(dtype).astype(np.float64)
    return np.moveaxis((codes * scale).reshape(v.shape), -1, axis)


WIDE = False


def mx_kscale(k):
    if not WIDE:
        return np.ones(k)
    levels = np.array([10, -10, 5, -5, 0])
    if k % 512:
        return np.exp2(np.random.permutation(np.resize(levels, k // 32))).repeat(32)
    a = np.empty((k // 512, 16))
    for p in range(k // 512):
        a[p, :8] = np.random.permutation(np.resize(levels, 8))
        for g in range(8):
            far = levels[np.abs(levels - a[p, g]) >= 10]
            a[p, g + 8] = far[np.random.randint(len(far))]
    return np.exp2(a.ravel()).repeat(32)


BF16 = ml_dtypes.bfloat16


def bf(x):
    return np.asarray(x, np.float32).astype(BF16)


def f64(x):
    return np.asarray(x).astype(np.float64)

def planes(Y):
    n, m = Y.shape
    b = f64(bf(Y)).reshape(n // 32, 32, m)
    amax = np.abs(b).max(1)
    byte = np.clip(np.where(amax > 0, np.frexp(amax)[1] - 1 + 127 - 7, 1), 1, 254)
    codes = (b * np.exp2(127.0 - byte)[:, None, :]).reshape(n, m).astype(np.float32).astype(ml_dtypes.float8_e4m3fn).view(np.uint8)
    words = codes.reshape(n // 512, 128, 4, m).transpose(0, 1, 3, 2)
    return np.ascontiguousarray(words), np.ascontiguousarray(byte.astype(np.uint8).reshape(n // 512, 16, m))


B, D, C, F, V = 256, 512, 3, 512, 1024
E = C * F
J = C * C * F
EPS = 1e-6


def unit_normals(nrm):
    sq = np.sum(nrm * nrm, axis=0, keepdims=True)
    return nrm / np.sqrt(sq + EPS)


def restrict_to_tangent(jac, n):
    along = np.sum(jac * n[None, None, :, :], axis=2, keepdims=True)
    return jac - along * n[None, None, :, :]


def setup_inputs():
    a = mx_kscale(D)
    t = mx_kscale(E)
    z = np.random.standard_normal((B, D)) * a
    w = np.random.standard_normal((D, J)) / np.sqrt(D) / a[:, None]
    b = 0.5 * np.random.standard_normal(J)
    nrm = 0.003 * np.random.standard_normal((C, F))
    g = (1.0 + 0.1 * np.random.standard_normal((C, F))) * t.reshape(C, F)
    s = (np.random.standard_normal((E, V)) + 0.5 * np.random.standard_normal((E, 1))) / np.sqrt(E) / t[:, None]
    return {"z": bf(z), "w": bf(w), "b": bf(b), "nrm": bf(nrm), "g": bf(g), "s": bf(s)}


def core(z, w, b, nrm, g, s):
    z, w, b, nrm, g, s = f64(z), f64(w), f64(b), f64(nrm), f64(g), f64(s)
    batch = z.shape[0]
    coords, faces = nrm.shape
    edge_dim, verts = s.shape

    h = (mxq(z, 1, "e4m3") @ mxq(w, 0, "e4m3")) + b
    jac = np.reshape(h, (batch, coords, coords, faces))

    n = unit_normals(nrm)

    t = restrict_to_tangent(jac, n)

    u = t * g[None, None, :, :]
    u = np.reshape(u, (batch * coords, edge_dim))

    y = mxq(u, 1, "e4m3") @ mxq(s, 0, "e4m3")
    y = np.reshape(y, (batch, coords, verts))

    return y - np.mean(y, axis=-1, keepdims=True)


def reference(z, w, b, nrm, g, s):
    R_out = core(z, w, b, nrm, g, s)
    words, scales = planes(np.moveaxis(R_out, 2, 0).reshape(1024, -1))
    return R_out, words, scales

@@ -1,0 +1,316 @@
+from contextlib import ExitStack
+
+import concourse.mybir as mybir
+from concourse.masks import make_identity
+
+F32 = mybir.dt.float32
+BF16 = mybir.dt.bfloat16
+U32 = mybir.dt.uint32
+I32 = mybir.dt.int32
+U8 = mybir.dt.uint8
+FP8X4 = mybir.dt.float8_e4m3fn_x4
+ACT = mybir.ActivationFunctionType
+ALU = mybir.AluOpType
+
+P = 128
+B, D, C, F, V = 256, 512, 3, 512, 1024
+E = C * F
+J = C * C * F
+FLOPS = 2 * B * D * J + 2 * B * C * E * V
+
+W_CHUNKS = ((0, 1), (1, 1), (2, 2), (4, 2), (6, 3))
+W_ON_SCALAR = (1, 3, 5, 7)
+S_ON_SCALAR = (0, 2, 4)
+HB = 128
+HM = C * HB
+
+
+def tile_neuraljacobianfieldpoissonintegration_x1_kernel(tc, z, w, b, nrm, g, s, out, words, scales):
+    nc = tc.nc
+    with ExitStack() as ctx:
+        keep = ctx.enter_context(tc.tile_pool(name="keep", bufs=1))
+        ring = ctx.enter_context(tc.tile_pool(name="ring", bufs=3))
+        psum = ctx.enter_context(tc.psum_pool(name="psum", bufs=1))
+
+        w_raw = []
+        for i, (blk, n) in enumerate(W_CHUNKS):
+            raw = keep.tile([P, 4, n * F], BF16, name="w_raw%d" % i)
+            w_raw.append(raw)
+        z_raw = keep.tile([P, 2, D], BF16, name="z_raw")
+        vec = keep.tile([P, F], BF16, name="vec")
+        nc.gpsimd.memset(vec[:], 0.0)
+
+        def load_w(i):
+            blk, n = W_CHUNKS[i]
+            nc.sync.dma_start(
+                out=w_raw[i][:],
+                in_=w[:, blk * F : (blk + n) * F].rearrange("(p j) c -> p j c", j=4),
+            )
+
+        load_w(0)
+        nc.scalar.dma_start(out=vec[0:3, :], in_=nrm)
+        nc.scalar.dma_start(out=vec[3:6, :], in_=g)
+        nc.scalar.dma_start(out=vec[6:15, :], in_=b.rearrange("(r f) -> r f", f=F))
+        load_w(1)
+        nc.sync.dma_start(out=z_raw[:], in_=z.rearrange("(r p) k -> p r k", p=P))
+        for i in range(2, len(W_CHUNKS)):
+            load_w(i)
+        s_raw = []
+        for k in range(C):
+            raw = keep.tile([P, 4, V], BF16, name="s_raw%d" % k)
+            nc.sync.dma_start(
+                out=raw[:], in_=s[k * F : (k + 1) * F, :].rearrange("(p j) v -> p j v", j=4)
+            )
+            s_raw.append(raw)
+
+        ident = keep.tile([P, P], F32, name="ident")
+        make_identity(nc, ident[:])
+        ident_bf = keep.tile([P, P], BF16, name="ident_bf")
+        nc.vector.tensor_copy(out=ident_bf[:], in_=ident[:])
+
+        vec_ps = psum.tile([P, 4, P], BF16, name="vec_ps", tag="mt", bufs=2)
+        for t in range(4):
+            nc.tensor.transpose(vec_ps[:, t, :], vec[:, t:F:4], ident_bf[:])
+        col = keep.tile([P, 15, 4], F32, name="col")
+        nc.vector.tensor_copy(out=col[:], in_=vec_ps[:, :, 0:15].rearrange("p t r -> p r t"))
+        nrm_c = col[:, 0:3, :]
+        g_c = col[:, 3:6, :]
+        sq = keep.tile([P, 3, 4], F32, name="sq")
+        nc.vector.tensor_mul(out=sq[:], in0=nrm_c, in1=nrm_c)
+        ss = keep.tile([P, 4], F32, name="ss")
+        nc.vector.tensor_add(out=ss[:], in0=sq[:, 0, :], in1=sq[:, 1, :])
+        ss2 = keep.tile([P, 4], F32, name="ss2")
+        nc.vector.scalar_tensor_tensor(
+            out=ss2[:], in0=ss[:], scalar=1e-6, in1=sq[:, 2, :], op0=ALU.add, op1=ALU.add
+        )
+        root = keep.tile([P, 4], F32, name="root")
+        nc.scalar.activation(out=root[:], in_=ss2[:], func=ACT.Sqrt)
+        rinv = keep.tile([P, 4], F32, name="rinv")
+        nc.vector.reciprocal(out=rinv[:], in_=root[:])
+        n_c = keep.tile([P, 3, 4], F32, name="n_c")
+        nc.vector.tensor_mul(out=n_c[:], in0=nrm_c, in1=rinv[:].unsqueeze(1).to_broadcast([P, 3, 4]))
+        ngn = keep.tile([P, 3, 4], F32, name="ngn")
+        nc.vector.scalar_tensor_tensor(
+            out=ngn[:], in0=n_c[:], scalar=-1.0, in1=g_c, op0=ALU.mult, op1=ALU.mult
+        )
+        gb = keep.tile([P, 3, 3, 4], F32, name="gb")
+        nb = keep.tile([P, 3, 3, 4], F32, name="nb")
+        for c in range(C):
+            b_c = col[:, 6 + 3 * c : 9 + 3 * c, :]
+            nc.vector.tensor_mul(out=gb[:, c], in0=b_c, in1=g_c)
+            nc.vector.tensor_mul(out=nb[:, c], in0=b_c, in1=n_c[:])
+        beta0 = keep.tile([P, 3, 4], F32, name="beta0")
+        nc.vector.tensor_add(out=beta0[:], in0=nb[:, :, 0, :], in1=nb[:, :, 1, :])
+        beta = keep.tile([P, 3, 4], F32, name="beta")
+        nc.vector.tensor_add(out=beta[:], in0=beta0[:], in1=nb[:, :, 2, :])
+
+        w_codes = keep.tile([P, J], U32, name="w_codes", align_bytes=64)
+        w_scales = keep.tile([P, J], U8, name="w_scales", align_bytes=64)
+
+        def w_block(blk):
+            for i, (b0, n) in enumerate(W_CHUNKS):
+                if b0 <= blk < b0 + n:
+                    src = w_raw[i][:, :, (blk - b0) * F : (blk - b0 + 1) * F]
+            grp = ring.tile([P, 4 * F], BF16, name="w_grp", align_bytes=64, bufs=4)
+            dst_v = grp[:].rearrange("p (t m j) -> p m j t", t=4, j=4)
+            src_v = src.rearrange("p j (m t) -> p m j t", t=4)
+            if blk in W_ON_SCALAR:
+                nc.scalar.copy(out=dst_v, in_=src_v)
+            else:
+                nc.vector.tensor_copy(out=dst_v, in_=src_v)
+            nc.vector.quantize_mx(
+                out=w_codes[:, blk * F : (blk + 1) * F].bitcast(FP8X4),
+                scales=w_scales[:, blk * F : (blk + 1) * F],
+                in_=grp[:],
+            )
+
+        z_codes = keep.tile([P, B], U32, name="z_codes", align_bytes=64)
+        z_scales = keep.tile([P, B], U8, name="z_scales", align_bytes=64)
+
+        def z_all():
+            zt = psum.tile([P, 2, B], F32, name="zt", tag="mt", bufs=2)
+            for r in range(2):
+                zw = z_raw[:, r, :].bitcast(F32)
+                for u in range(2):
+                    nc.tensor.transpose(zt[:, u, r * P : (r + 1) * P], zw[:, u : D // 2 : 2], ident[:])
+            z_grp = keep.tile([P, 4 * B], BF16, name="z_grp", align_bytes=64)
+            nc.vector.tensor_copy(
+                out=z_grp[:].bitcast(F32).rearrange("p (m u) -> p m u", u=2),
+                in_=zt[:].rearrange("p u m -> p m u"),
+            )
+            nc.vector.quantize_mx(out=z_codes[:].bitcast(FP8X4), scales=z_scales[:], in_=z_grp[:])
+
+        for blk in range(2):
+            w_block(blk)
+        z_all()
+        for blk in range(2, 9):
+            w_block(blk)
+
+        s_codes = keep.tile([P, C * V], U32, name="s_codes", align_bytes=64)
+        s_scales = keep.tile([P, C * V], U8, name="s_scales", align_bytes=64)
+
+        def s_piece(q):
+            k, vh = divmod(q, 2)
+            grp = ring.tile([P, 4 * F], BF16, name="s_grp", align_bytes=64, bufs=3)
+            dst_v = grp[:].rearrange("p (c i t) -> p c t i", i=4, t=4)
+            src_v = s_raw[k][:, :, vh * 512 : (vh + 1) * 512].rearrange("p t (c i) -> p c t i", i=4)
+            if q in S_ON_SCALAR:
+                nc.scalar.copy(out=dst_v, in_=src_v)
+            else:
+                nc.vector.tensor_copy(out=dst_v, in_=src_v)
+            nc.vector.quantize_mx(
+                out=s_codes[:, q * 512 : (q + 1) * 512].bitcast(FP8X4),
+                scales=s_scales[:, q * 512 : (q + 1) * 512],
+                in_=grp[:],
+            )
+
+        u_t = [
+            [keep.tile([P, 4, C, HB], BF16, name="u_t%d_%d" % (h, k)) for k in range(C)]
+            for h in range(2)
+        ]
+
+        def unit(h, t):
+            hp = []
+            for k in range(C):
+                hk = psum.tile([P, C, HB], F32, name="hk", tag="h", bufs=4)
+                for c in range(C):
+                    col0 = (c * C + k) * F + t * P
+                    nc.tensor.matmul_mx(
+                        out=hk[:, c, :],
+                        lhsT=w_codes[:, col0 : col0 + P].bitcast(FP8X4),
+                        lhsT_scale=w_scales[:, col0 : col0 + P],
+                        rhs=z_codes[:, h * HB : (h + 1) * HB].bitcast(FP8X4),
+                        rhs_scale=z_scales[:, h * HB : (h + 1) * HB],
+                        start=True,
+                        stop=True,
+                    )
+                hp.append(hk)
+            y0 = ring.tile([P, C, HB], F32, name="y0")
+            for c in range(C):
+                nc.scalar.activation(
+                    out=y0[:, c, :], in_=hp[0][:, c, :], func=ACT.Identity,
+                    scale=n_c[:, 0, t : t + 1], bias=beta[:, c, t : t + 1],
+                )
+            a1 = ring.tile([P, C, HB], F32, name="a1")
+            nc.vector.scalar_tensor_tensor(
+                out=a1[:], in0=hp[1][:], scalar=n_c[:, 1, t : t + 1], in1=y0[:], op0=ALU.mult, op1=ALU.add
+            )
+            a2 = ring.tile([P, C, HB], F32, name="a2")
+            nc.vector.scalar_tensor_tensor(
+                out=a2[:], in0=hp[2][:], scalar=n_c[:, 2, t : t + 1], in1=a1[:], op0=ALU.mult, op1=ALU.add
+            )
+            for k in range(C):
+                pk = ring.tile([P, C, HB], F32, name="pk", bufs=6)
+                for c in range(C):
+                    nc.scalar.activation(
+                        out=pk[:, c, :], in_=hp[k][:, c, :], func=ACT.Identity,
+                        scale=col[:, 3 + k, t : t + 1], bias=gb[:, c, k, t : t + 1],
+                    )
+                nc.vector.scalar_tensor_tensor(
+                    out=u_t[h][k][:, t], in0=a2[:], scalar=ngn[:, k, t : t + 1], in1=pk[:],
+                    op0=ALU.mult, op1=ALU.add,
+                )
+
+        u_codes = [keep.tile([P, C * HM], U32, name="u_codes%d" % h, align_bytes=64) for h in range(2)]
+        u_scales = [keep.tile([P, C * HM], U8, name="u_scales%d" % h, align_bytes=64) for h in range(2)]
+
+        def pack_u(h):
+            for k in range(C):
+                grp = ring.tile([P, 4 * HM], BF16, name="u_grp", align_bytes=64)
+                for half in range(2):
+                    up = psum.tile([P, 2 * HM], BF16, name="up", tag="mt", bufs=2)
+                    for q in range(2):
+                        b0 = (2 * half + q) * 32
+                        nc.tensor.matmul(
+                            up[:, q * HM : (q + 1) * HM].rearrange("p (b c t) -> p b c t", c=C, t=4),
+                            ident_bf[:],
+                            u_t[h][k][:, :, :, b0 : b0 + 32].rearrange("p t c b -> p b c t"),
+                            start=True,
+                            stop=True,
+                        )
+                    nc.scalar.copy(out=grp[:, half * 2 * HM : (half + 1) * 2 * HM], in_=up[:])
+                for m0, n in ((0, 256), (256, 128)):
+                    nc.vector.quantize_mx(
+                        out=u_codes[h][:, k * HM + m0 : k * HM + m0 + n].bitcast(FP8X4),
+                        scales=u_scales[h][:, k * HM + m0 : k * HM + m0 + n],
+                        in_=grp[:, 4 * m0 : 4 * (m0 + n)],
+                    )
+
+        out_rows = out.rearrange("b c v -> (b c) v")
+        words_i = words.bitcast(I32).rearrange("g p m t -> p g (m t)")
+        scales_i = scales.bitcast(I32)
+        p_scales = keep.tile([P, 2, C * B], U8, name="p_scales", align_bytes=64)
+
+        def m_tile(h, i):
+            raw = ring.tile([P, V], F32, name="raw")
+            sums = ring.tile([P, 2], F32, name="sums")
+            for vh in range(2):
+                y = psum.tile([P, 512], F32, name="y", tag="y", bufs=2)
+                for k in range(C):
+                    ucol = k * HM + i * P
+                    scol = k * V + vh * 512
+                    nc.tensor.matmul_mx(
+                        out=y[:],
+                        lhsT=u_codes[h][:, ucol : ucol + P].bitcast(FP8X4),
+                        lhsT_scale=u_scales[h][:, ucol : ucol + P],
+                        rhs=s_codes[:, scol : scol + 512].bitcast(FP8X4),
+                        rhs_scale=s_scales[:, scol : scol + 512],
+                        start=(k == 0),
+                        stop=(k == C - 1),
+                    )
+                nc.scalar.activation(
+                    out=raw[:, vh * 512 : (vh + 1) * 512], in_=y[:], func=ACT.Identity,
+                    accum_out=sums[:, vh : vh + 1],
+                )
+            nm = ring.tile([P, 1], F32, name="nm")
+            nc.vector.tensor_scalar(
+                out=nm[:], in0=sums[:, 0:1], scalar1=sums[:, 1:2], scalar2=-1.0 / V, op0=ALU.add, op1=ALU.mult
+            )
+            cb = ring.tile([P, V], BF16, name="cb")
+            nc.vector.tensor_scalar(out=cb[:], in0=raw[:], scalar1=nm[:], scalar2=None, op0=ALU.add)
+            cent = ring.tile([P, V], F32, name="cent")
+            nc.vector.tensor_scalar(out=cent[:], in0=raw[:], scalar1=nm[:], scalar2=None, op0=ALU.add)
+            m0 = h * HM + i * P
+            nc.sync.dma_start(out=out_rows[m0 : m0 + P, :], in_=cent[:])
+            tp = psum.tile([P, 2, 2, P], F32, name="tp", tag="mt", bufs=2)
+            cw = cb[:].bitcast(F32)
+            for gr in range(2):
+                for u in range(2):
+                    nc.tensor.transpose(
+                        tp[:, gr, u, :], cw[:, 256 * gr + u : 256 * (gr + 1) : 2], ident[:]
+                    )
+            qin = ring.tile([P, 2 * 4 * P], BF16, name="qin", align_bytes=64)
+            nc.scalar.copy(
+                out=qin[:].bitcast(F32).rearrange("p (g m u) -> p g m u", g=2, u=2),
+                in_=tp[:].rearrange("p g u m -> p g m u"),
+            )
+            codes = ring.tile([P, 2, P], U32, name="codes", align_bytes=64)
+            for gr in range(2):
+                nc.vector.quantize_mx(
+                    out=codes[:, gr, :].bitcast(FP8X4),
+                    scales=p_scales[:, gr, m0 : m0 + P],
+                    in_=qin[:, gr * 512 : (gr + 1) * 512],
+                )
+            nc.sync.dma_start(out=words_i[:, :, m0 : m0 + P], in_=codes[:].bitcast(I32))
+
+        def store_scales(h):
+            for q in range(4):
+                nc.sync.dma_start(
+                    out=scales_i[:, 4 * q : 4 * q + 4, h * 96 : (h + 1) * 96].rearrange("g r m -> r g m"),
+                    in_=p_scales[32 * q : 32 * q + 4, :, h * HM : (h + 1) * HM].bitcast(I32),
+                )
+
+        for t in range(4):
+            unit(0, t)
+        for q in range(6):
+            s_piece(q)
+        pack_u(0)
+        for i in range(3):
+            m_tile(0, i)
+        store_scales(0)
+        for t in range(4):
+            unit(1, t)
+        pack_u(1)
+        for i in range(3):
+            m_tile(1, i)
+        store_scales(1)

@@ -17,300 +17,438 @@ B, D, C, F, V = 256, 512, 3, 512, 1024
 E = C * F
 J = C * C * F
 FLOPS = 2 * B * D * J + 2 * B * C * E * V
+LOADS = "w:0:1 v w:1:1 z w:2:1 s:0 s:1 s:2 w:3:3 w:6:3"
+ORDER = "W 0, W 1, W 2, V, Z, B 0 0, B 0 1, K 0, S 0, S 1, S 2, S 3, S 4, S 5, W 3, W 4, W 5, B 1 0, B 1 1, K 1, C 0 0, C 0 1, W 6, W 7, W 8, B 2 0, B 2 1, K 2, C 1 0, C 1 1, C 2 0, R 0, C 2 1, R 1"
 
-W_CHUNKS = ((0, 1), (1, 1), (2, 2), (4, 2), (6, 3))
-W_ON_SCALAR = (1, 3, 5, 7)
-S_ON_SCALAR = (0, 2, 4)
-HB = 128
-HM = C * HB
+LATENCY = {"V": 70, "S": 70, "P": 110, "D": 1700, "G": 150}
+
+
+def list_schedule(tasks):
+    writer, readers = {}, {}
+    after = []
+    for i, (costs, reads, writes, emit) in enumerate(tasks):
+        need = set()
+        for r in reads:
+            if r in writer:
+                need.add(writer[r])
+        for r in writes:
+            if r in writer:
+                need.add(writer[r])
+            for j in readers.get(r, []):
+                need.add(j)
+        for r in reads:
+            readers.setdefault(r, []).append(i)
+        for r in writes:
+            writer[r] = i
+            readers[r] = []
+        after.append(need)
+    free = {}
+    for costs, reads, writes, emit in tasks:
+        for e in costs:
+            free[e] = 0
+    done = {}
+    left = list(range(len(tasks)))
+    order = []
+    while left:
+        best = None
+        for i in left:
+            if not all([j in done for j in after[i]]):
+                continue
+            costs = tasks[i][0]
+            for e in costs:
+                ready = free[e]
+                for j in after[i]:
+                    end, by = done[j]
+                    lag = LATENCY[by] + (90 if by == "V" and e == "V" else 0)
+                    if by == e and e in ("P",):
+                        lag = 0
+                    ready = max(ready, end + lag)
+                key = (ready, i, costs[e])
+                if best is None or key < best[0]:
+                    best = (key, i, e)
+        key, i, e = best
+        done[i] = (key[0] + tasks[i][0][e], e)
+        free[e] = key[0] + tasks[i][0][e]
+        left.remove(i)
+        order.append((key[0], e, i))
+    return sorted(order)
 
 
 def tile_neuraljacobianfieldpoissonintegration_x1_kernel(tc, z, w, b, nrm, g, s, out, words, scales):
     nc = tc.nc
     with ExitStack() as ctx:
         keep = ctx.enter_context(tc.tile_pool(name="keep", bufs=1))
-        ring = ctx.enter_context(tc.tile_pool(name="ring", bufs=3))
         psum = ctx.enter_context(tc.psum_pool(name="psum", bufs=1))
 
-        w_raw = []
-        for i, (blk, n) in enumerate(W_CHUNKS):
-            raw = keep.tile([P, 4, n * F], BF16, name="w_raw%d" % i)
-            w_raw.append(raw)
-        z_raw = keep.tile([P, 2, D], BF16, name="z_raw")
-        vec = keep.tile([P, F], BF16, name="vec")
+        def bank(name):
+            return psum.tile([P, 512], F32, name=name)
+
+        h_ps = [bank("h%d" % i) for i in range(4)]
+        y_ps = [bank("y%d" % i) for i in range(2)]
+        m_ps = [bank("m%d" % i) for i in range(2)]
+
+        def sb(name, shape, dt, n=None):
+            if n is None:
+                return keep.tile([P] + shape, dt, name=name, align_bytes=64)
+            return [keep.tile([P] + shape, dt, name="%s%d" % (name, i), align_bytes=64) for i in range(n)]
+
+        tasks = []
+
+        def task(costs, reads, writes, emit):
+            tasks.append((costs, reads, writes, emit))
+
+        turns = {}
+
+        def ring(name, n):
+            turns[name] = turns.get(name, -1) + 1
+            return turns[name] % n
+
+        ident = sb("ident", [P], F32)
+        ident_bf = sb("ident_bf", [P], BF16)
+        vec = sb("vec", [F], BF16)
         nc.gpsimd.memset(vec[:], 0.0)
-
-        def load_w(i):
-            blk, n = W_CHUNKS[i]
-            nc.sync.dma_start(
-                out=w_raw[i][:],
-                in_=w[:, blk * F : (blk + n) * F].rearrange("(p j) c -> p j c", j=4),
-            )
-
-        load_w(0)
-        nc.scalar.dma_start(out=vec[0:3, :], in_=nrm)
-        nc.scalar.dma_start(out=vec[3:6, :], in_=g)
-        nc.scalar.dma_start(out=vec[6:15, :], in_=b.rearrange("(r f) -> r f", f=F))
-        load_w(1)
-        nc.sync.dma_start(out=z_raw[:], in_=z.rearrange("(r p) k -> p r k", p=P))
-        for i in range(2, len(W_CHUNKS)):
-            load_w(i)
-        s_raw = []
-        for k in range(C):
-            raw = keep.tile([P, 4, V], BF16, name="s_raw%d" % k)
-            nc.sync.dma_start(
-                out=raw[:], in_=s[k * F : (k + 1) * F, :].rearrange("(p j) v -> p j v", j=4)
-            )
-            s_raw.append(raw)
-
-        ident = keep.tile([P, P], F32, name="ident")
         make_identity(nc, ident[:])
-        ident_bf = keep.tile([P, P], BF16, name="ident_bf")
-        nc.vector.tensor_copy(out=ident_bf[:], in_=ident[:])
+        nc.gpsimd.tensor_copy(out=ident_bf[:], in_=ident[:])
 
-        vec_ps = psum.tile([P, 4, P], BF16, name="vec_ps", tag="mt", bufs=2)
-        for t in range(4):
-            nc.tensor.transpose(vec_ps[:, t, :], vec[:, t:F:4], ident_bf[:])
-        col = keep.tile([P, 15, 4], F32, name="col")
-        nc.vector.tensor_copy(out=col[:], in_=vec_ps[:, :, 0:15].rearrange("p t r -> p r t"))
+        w_raw = {}
+        z_raw = sb("z_raw", [2, D], BF16)
+        s_raw = sb("s_raw", [4, V], BF16, C)
+
+        def load_w(b0, n):
+            raw = sb("w_raw%d" % b0, [4, n * F], BF16)
+            for i in range(n):
+                w_raw[b0 + i] = (raw, i, b0)
+            nc.sync.dma_start(out=raw[:], in_=w[:, b0 * F : (b0 + n) * F].rearrange("(p j) c -> p j c", j=4))
+            task({"D": n * 880}, [], [("wraw", b0)], None)
+
+        def load_s(k):
+            nc.sync.dma_start(out=s_raw[k][:], in_=s[k * F : (k + 1) * F, :].rearrange("(p j) v -> p j v", j=4))
+            task({"D": 1760}, [], [("sraw", k)], None)
+
+        def load_z():
+            nc.sync.dma_start(out=z_raw[:], in_=z.rearrange("(r p) k -> p r k", p=P))
+            task({"D": 440}, [], ["zraw"], None)
+
+        def load_v():
+            nc.scalar.dma_start(out=vec[0:3, :], in_=nrm)
+            nc.scalar.dma_start(out=vec[3:6, :], in_=g)
+            nc.scalar.dma_start(out=vec[6:15, :], in_=b.rearrange("(r f) -> r f", f=F))
+            task({"D": 340}, [], ["vec"], None)
+
+        task({"D": 900}, [], ["start"], None)
+        loaders = {"w": load_w, "s": load_s, "z": load_z, "v": load_v}
+        for item in LOADS.split():
+            parts = item.split(":")
+            loaders[parts[0]](*[int(x) for x in parts[1:]])
+
+        col = sb("col", [15, 4], F32)
+        sq = sb("sq", [3, 4], F32)
+        ss = sb("ss", [4], F32)
+        ss2 = sb("ss2", [4], F32)
+        root = sb("root", [4], F32)
+        rinv = sb("rinv", [4], F32)
+        n_c = sb("n_c", [3, 4], F32)
+        ngn = sb("ngn", [3, 4], F32)
+        gb = sb("gb", [3, 3, 4], F32)
+        nb = sb("nb", [3, 3, 4], F32)
+        beta0 = sb("beta0", [3, 4], F32)
+        beta = sb("beta", [3, 4], F32)
         nrm_c = col[:, 0:3, :]
         g_c = col[:, 3:6, :]
-        sq = keep.tile([P, 3, 4], F32, name="sq")
-        nc.vector.tensor_mul(out=sq[:], in0=nrm_c, in1=nrm_c)
-        ss = keep.tile([P, 4], F32, name="ss")
-        nc.vector.tensor_add(out=ss[:], in0=sq[:, 0, :], in1=sq[:, 1, :])
-        ss2 = keep.tile([P, 4], F32, name="ss2")
-        nc.vector.scalar_tensor_tensor(
-            out=ss2[:], in0=ss[:], scalar=1e-6, in1=sq[:, 2, :], op0=ALU.add, op1=ALU.add
-        )
-        root = keep.tile([P, 4], F32, name="root")
-        nc.scalar.activation(out=root[:], in_=ss2[:], func=ACT.Sqrt)
-        rinv = keep.tile([P, 4], F32, name="rinv")
-        nc.vector.reciprocal(out=rinv[:], in_=root[:])
-        n_c = keep.tile([P, 3, 4], F32, name="n_c")
-        nc.vector.tensor_mul(out=n_c[:], in0=nrm_c, in1=rinv[:].unsqueeze(1).to_broadcast([P, 3, 4]))
-        ngn = keep.tile([P, 3, 4], F32, name="ngn")
-        nc.vector.scalar_tensor_tensor(
-            out=ngn[:], in0=n_c[:], scalar=-1.0, in1=g_c, op0=ALU.mult, op1=ALU.mult
-        )
-        gb = keep.tile([P, 3, 3, 4], F32, name="gb")
-        nb = keep.tile([P, 3, 3, 4], F32, name="nb")
-        for c in range(C):
-            b_c = col[:, 6 + 3 * c : 9 + 3 * c, :]
-            nc.vector.tensor_mul(out=gb[:, c], in0=b_c, in1=g_c)
-            nc.vector.tensor_mul(out=nb[:, c], in0=b_c, in1=n_c[:])
-        beta0 = keep.tile([P, 3, 4], F32, name="beta0")
-        nc.vector.tensor_add(out=beta0[:], in0=nb[:, :, 0, :], in1=nb[:, :, 1, :])
-        beta = keep.tile([P, 3, 4], F32, name="beta")
-        nc.vector.tensor_add(out=beta[:], in0=beta0[:], in1=nb[:, :, 2, :])
 
-        w_codes = keep.tile([P, J], U32, name="w_codes", align_bytes=64)
-        w_scales = keep.tile([P, J], U8, name="w_scales", align_bytes=64)
+        def coef():
+            i = ring("m", 2)
+            ps = m_ps[i][:].bitcast(BF16)
+
+            def turn(e):
+                for t in range(4):
+                    nc.tensor.transpose(ps[:, t * P : (t + 1) * P], vec[:, t:F:4], ident_bf[:])
+
+            task({"P": 420}, ["vec"], [("m", i)], turn)
+
+            def v1(e):
+                nc.vector.tensor_copy(
+                    out=col[:], in_=ps[:, 0 : 4 * P].rearrange("p (t r) -> p t r", t=4)[:, :, 0:15].rearrange("p t r -> p r t")
+                )
+
+            task({"V": 80}, [("m", i)], ["col"], v1)
+            task({"V": 70}, ["col"], ["sq"], lambda e: nc.vector.tensor_mul(out=sq[:], in0=nrm_c, in1=nrm_c))
+            task({"V": 70}, ["sq"], ["ss"], lambda e: nc.vector.tensor_add(out=ss[:], in0=sq[:, 0, :], in1=sq[:, 1, :]))
+            task({"V": 70}, ["sq", "ss"], ["ss2"], lambda e: nc.vector.scalar_tensor_tensor(
+                out=ss2[:], in0=ss[:], scalar=1e-6, in1=sq[:, 2, :], op0=ALU.add, op1=ALU.add))
+            task({"S": 80}, ["ss2"], ["root"], lambda e: nc.scalar.activation(out=root[:], in_=ss2[:], func=ACT.Sqrt))
+            task({"V": 80}, ["root"], ["rinv"], lambda e: nc.vector.reciprocal(out=rinv[:], in_=root[:]))
+            task({"V": 70}, ["rinv", "col"], ["n_c"], lambda e: nc.vector.tensor_mul(
+                out=n_c[:], in0=nrm_c, in1=rinv[:].unsqueeze(1).to_broadcast([P, 3, 4])))
+            task({"V": 70}, ["n_c", "col"], ["ngn"], lambda e: nc.vector.scalar_tensor_tensor(
+                out=ngn[:], in0=n_c[:], scalar=-1.0, in1=g_c, op0=ALU.mult, op1=ALU.mult))
+
+            def products(dst, src, c):
+                return lambda e: nc.vector.tensor_mul(out=dst[:, c], in0=col[:, 6 + 3 * c : 9 + 3 * c, :], in1=src)
+
+            for c in range(C):
+                task({"V": 70}, ["col"], [("gb", c)], products(gb, g_c, c))
+                task({"V": 70}, ["col", "n_c"], [("nb", c)], products(nb, n_c[:], c))
+            task({"V": 70}, [("nb", 0), ("nb", 1), ("nb", 2)], ["beta0"], lambda e: nc.vector.tensor_add(
+                out=beta0[:], in0=nb[:, :, 0, :], in1=nb[:, :, 1, :]))
+            task({"V": 70}, ["beta0"], ["coef"], lambda e: nc.vector.tensor_add(out=beta[:], in0=beta0[:], in1=nb[:, :, 2, :]))
+
+        def copy_on(e, dst, src):
+            if e == "S":
+                nc.scalar.copy(out=dst, in_=src)
+            elif e == "G":
+                nc.gpsimd.tensor_copy(out=dst, in_=src)
+            else:
+                nc.vector.tensor_copy(out=dst, in_=src)
+
+        w_codes = sb("w_codes", [J], U32)
+        w_scales = sb("w_scales", [J], U8)
+        w_grp = sb("w_grp", [4 * F], BF16, 3)
+
+        def quant(codes, scale, src):
+            return lambda e: nc.vector.quantize_mx(out=codes.bitcast(FP8X4), scales=scale, in_=src)
 
         def w_block(blk):
-            for i, (b0, n) in enumerate(W_CHUNKS):
-                if b0 <= blk < b0 + n:
-                    src = w_raw[i][:, :, (blk - b0) * F : (blk - b0 + 1) * F]
-            grp = ring.tile([P, 4 * F], BF16, name="w_grp", align_bytes=64, bufs=4)
-            dst_v = grp[:].rearrange("p (t m j) -> p m j t", t=4, j=4)
-            src_v = src.rearrange("p j (m t) -> p m j t", t=4)
-            if blk in W_ON_SCALAR:
-                nc.scalar.copy(out=dst_v, in_=src_v)
-            else:
-                nc.vector.tensor_copy(out=dst_v, in_=src_v)
-            nc.vector.quantize_mx(
-                out=w_codes[:, blk * F : (blk + 1) * F].bitcast(FP8X4),
-                scales=w_scales[:, blk * F : (blk + 1) * F],
-                in_=grp[:],
-            )
+            raw, i, b0 = w_raw[blk]
+            r = ring("w", 3)
+            grp = w_grp[r]
 
-        z_codes = keep.tile([P, B], U32, name="z_codes", align_bytes=64)
-        z_scales = keep.tile([P, B], U8, name="z_scales", align_bytes=64)
+            def half(h):
+                m0 = 64 * h
+                dst = grp[:].rearrange("p (t m j) -> p m t j", t=4, j=4)[:, m0 : m0 + 64]
+                src = raw[:, :, i * F : (i + 1) * F].rearrange("p j (m t) -> p m t j", t=4)[:, m0 : m0 + 64]
+                return lambda e: copy_on(e, dst, src)
+
+            for h in range(2):
+                task({"V": 530, "S": 1000}, [("wraw", b0)], [("wg", r, h)], half(h))
+            cols = slice(blk * F, (blk + 1) * F)
+            task({"V": 465}, [("wg", r, 0), ("wg", r, 1)], [("wc", blk)], quant(w_codes[:, cols], w_scales[:, cols], grp[:]))
+
+        z_codes = sb("z_codes", [B], U32)
+        z_scales = sb("z_scales", [B], U8)
+        z_grp = sb("z_grp", [4 * B], BF16)
 
         def z_all():
-            zt = psum.tile([P, 2, B], F32, name="zt", tag="mt", bufs=2)
-            for r in range(2):
-                zw = z_raw[:, r, :].bitcast(F32)
-                for u in range(2):
-                    nc.tensor.transpose(zt[:, u, r * P : (r + 1) * P], zw[:, u : D // 2 : 2], ident[:])
-            z_grp = keep.tile([P, 4 * B], BF16, name="z_grp", align_bytes=64)
-            nc.vector.tensor_copy(
-                out=z_grp[:].bitcast(F32).rearrange("p (m u) -> p m u", u=2),
-                in_=zt[:].rearrange("p u m -> p m u"),
-            )
-            nc.vector.quantize_mx(out=z_codes[:].bitcast(FP8X4), scales=z_scales[:], in_=z_grp[:])
+            i = ring("m", 2)
+            zt = m_ps[i][:].rearrange("p (u m) -> p u m", u=2)
 
-        for blk in range(2):
-            w_block(blk)
-        z_all()
-        for blk in range(2, 9):
-            w_block(blk)
+            def turn(e):
+                for r in range(2):
+                    zw = z_raw[:, r, :].bitcast(F32)
+                    for u in range(2):
+                        nc.tensor.transpose(zt[:, u, r * P : (r + 1) * P], zw[:, u : D // 2 : 2], ident[:])
 
-        s_codes = keep.tile([P, C * V], U32, name="s_codes", align_bytes=64)
-        s_scales = keep.tile([P, C * V], U8, name="s_scales", align_bytes=64)
+            task({"P": 450}, ["zraw"], [("m", i)], turn)
+            task({"V": 440}, [("m", i)], ["zg"], lambda e: nc.vector.tensor_copy(
+                out=z_grp[:].bitcast(F32).rearrange("p (m u) -> p m u", u=2), in_=zt.rearrange("p u m -> p m u")))
+            task({"V": 240}, ["zg"], ["zc"], quant(z_codes[:], z_scales[:], z_grp[:]))
+
+        s_codes = sb("s_codes", [C * V], U32)
+        s_scales = sb("s_scales", [C * V], U8)
+        s_grp = sb("s_grp", [4 * 512], BF16, 3)
 
         def s_piece(q):
             k, vh = divmod(q, 2)
-            grp = ring.tile([P, 4 * F], BF16, name="s_grp", align_bytes=64, bufs=3)
-            dst_v = grp[:].rearrange("p (c i t) -> p c t i", i=4, t=4)
-            src_v = s_raw[k][:, :, vh * 512 : (vh + 1) * 512].rearrange("p t (c i) -> p c t i", i=4)
-            if q in S_ON_SCALAR:
-                nc.scalar.copy(out=dst_v, in_=src_v)
-            else:
-                nc.vector.tensor_copy(out=dst_v, in_=src_v)
-            nc.vector.quantize_mx(
-                out=s_codes[:, q * 512 : (q + 1) * 512].bitcast(FP8X4),
-                scales=s_scales[:, q * 512 : (q + 1) * 512],
-                in_=grp[:],
-            )
+            r = ring("s", 3)
 
-        u_t = [
-            [keep.tile([P, 4, C, HB], BF16, name="u_t%d_%d" % (h, k)) for k in range(C)]
-            for h in range(2)
-        ]
+            def half(h):
+                v0 = 256 * h
+                dst = s_grp[r][:].rearrange("p (c t) -> p c t", t=4)[:, v0 : v0 + 256]
+                src = s_raw[k][:, :, vh * 512 + v0 : vh * 512 + v0 + 256].rearrange("p t c -> p c t")
+                return lambda e: copy_on(e, dst, src)
 
-        def unit(h, t):
-            hp = []
+            for h in range(2):
+                task({"V": 530, "S": 1000}, [("sraw", k)], [("sg", r, h)], half(h))
+            cols = slice(q * 512, (q + 1) * 512)
+            task({"V": 465}, [("sg", r, 0), ("sg", r, 1)], [("sc", q)], quant(s_codes[:, cols], s_scales[:, cols], s_grp[r][:]))
+
+        u_t = sb("u_t", [4, C, B], BF16, 2)
+        y0 = sb("y0_", [B], F32, 4)
+        a1 = sb("a1_", [B], F32, 4)
+        a2 = sb("a2_", [B], F32, 4)
+        pk = sb("pk_", [B], F32, 8)
+
+        coefs = ["coef", "ngn", ("gb", 0), ("gb", 1), ("gb", 2)]
+
+        def stt(dst, in0, scalar, in1):
+            return lambda e: nc.vector.scalar_tensor_tensor(out=dst, in0=in0, scalar=scalar, in1=in1, op0=ALU.mult, op1=ALU.add)
+
+        def affine(dst, src, scale, bias):
+            return lambda e: nc.scalar.activation(out=dst, in_=src, func=ACT.Identity, scale=scale, bias=bias)
+
+        def stage1(c, tp):
+            banks = []
             for k in range(C):
-                hk = psum.tile([P, C, HB], F32, name="hk", tag="h", bufs=4)
-                for c in range(C):
-                    col0 = (c * C + k) * F + t * P
-                    nc.tensor.matmul_mx(
-                        out=hk[:, c, :],
-                        lhsT=w_codes[:, col0 : col0 + P].bitcast(FP8X4),
-                        lhsT_scale=w_scales[:, col0 : col0 + P],
-                        rhs=z_codes[:, h * HB : (h + 1) * HB].bitcast(FP8X4),
-                        rhs_scale=z_scales[:, h * HB : (h + 1) * HB],
-                        start=True,
-                        stop=True,
-                    )
-                hp.append(hk)
-            y0 = ring.tile([P, C, HB], F32, name="y0")
-            for c in range(C):
-                nc.scalar.activation(
-                    out=y0[:, c, :], in_=hp[0][:, c, :], func=ACT.Identity,
-                    scale=n_c[:, 0, t : t + 1], bias=beta[:, c, t : t + 1],
-                )
-            a1 = ring.tile([P, C, HB], F32, name="a1")
-            nc.vector.scalar_tensor_tensor(
-                out=a1[:], in0=hp[1][:], scalar=n_c[:, 1, t : t + 1], in1=y0[:], op0=ALU.mult, op1=ALU.add
-            )
-            a2 = ring.tile([P, C, HB], F32, name="a2")
-            nc.vector.scalar_tensor_tensor(
-                out=a2[:], in0=hp[2][:], scalar=n_c[:, 2, t : t + 1], in1=a1[:], op0=ALU.mult, op1=ALU.add
-            )
-            for k in range(C):
-                pk = ring.tile([P, C, HB], F32, name="pk", bufs=6)
-                for c in range(C):
-                    nc.scalar.activation(
-                        out=pk[:, c, :], in_=hp[k][:, c, :], func=ACT.Identity,
-                        scale=col[:, 3 + k, t : t + 1], bias=gb[:, c, k, t : t + 1],
-                    )
-                nc.vector.scalar_tensor_tensor(
-                    out=u_t[h][k][:, t], in0=a2[:], scalar=ngn[:, k, t : t + 1], in1=pk[:],
-                    op0=ALU.mult, op1=ALU.add,
-                )
+                i = ring("h", 4)
+                banks.append(i)
 
-        u_codes = [keep.tile([P, C * HM], U32, name="u_codes%d" % h, align_bytes=64) for h in range(2)]
-        u_scales = [keep.tile([P, C * HM], U8, name="u_scales%d" % h, align_bytes=64) for h in range(2)]
-
-        def pack_u(h):
-            for k in range(C):
-                grp = ring.tile([P, 4 * HM], BF16, name="u_grp", align_bytes=64)
-                for half in range(2):
-                    up = psum.tile([P, 2 * HM], BF16, name="up", tag="mt", bufs=2)
-                    for q in range(2):
-                        b0 = (2 * half + q) * 32
-                        nc.tensor.matmul(
-                            up[:, q * HM : (q + 1) * HM].rearrange("p (b c t) -> p b c t", c=C, t=4),
-                            ident_bf[:],
-                            u_t[h][k][:, :, :, b0 : b0 + 32].rearrange("p t c b -> p b c t"),
+                def mm(e, k=k, i=i):
+                    for d in range(2):
+                        col0 = (c * C + k) * F + (2 * tp + d) * P
+                        nc.tensor.matmul_mx(
+                            out=h_ps[i][:, d * B : (d + 1) * B],
+                            lhsT=w_codes[:, col0 : col0 + P].bitcast(FP8X4),
+                            lhsT_scale=w_scales[:, col0 : col0 + P],
+                            rhs=z_codes[:].bitcast(FP8X4),
+                            rhs_scale=z_scales[:],
                             start=True,
                             stop=True,
                         )
-                    nc.scalar.copy(out=grp[:, half * 2 * HM : (half + 1) * 2 * HM], in_=up[:])
-                for m0, n in ((0, 256), (256, 128)):
-                    nc.vector.quantize_mx(
-                        out=u_codes[h][:, k * HM + m0 : k * HM + m0 + n].bitcast(FP8X4),
-                        scales=u_scales[h][:, k * HM + m0 : k * HM + m0 + n],
-                        in_=grp[:, 4 * m0 : 4 * (m0 + n)],
-                    )
 
-        out_rows = out.rearrange("b c v -> (b c) v")
+                task({"P": 230}, ["zc", ("wc", c * C + k)], [("h", i)], mm)
+            ry, r1, r2 = [[ring(n, 4) for d in range(2)] for n in ("y0", "a1", "a2")]
+
+            def hv(k, d):
+                return h_ps[banks[k]][:, d * B : (d + 1) * B]
+
+            for d in range(2):
+                t = 2 * tp + d
+                task({"S": 225}, [("h", banks[0])] + coefs, [("y0", ry[d])],
+                     affine(y0[ry[d]][:], hv(0, d), n_c[:, 0, t : t + 1], beta[:, c, t : t + 1]))
+            for d in range(2):
+                t = 2 * tp + d
+                task({"V": 230}, [("h", banks[1]), ("y0", ry[d])] + coefs, [("a1", r1[d])],
+                     stt(a1[r1[d]][:], hv(1, d), n_c[:, 1, t : t + 1], y0[ry[d]][:]))
+            for d in range(2):
+                t = 2 * tp + d
+                task({"V": 230}, [("h", banks[2]), ("a1", r1[d])], [("a2", r2[d])],
+                     stt(a2[r2[d]][:], hv(2, d), n_c[:, 2, t : t + 1], a1[r1[d]][:]))
+            for k in range(C):
+                for d in range(2):
+                    t = 2 * tp + d
+                    r = ring("pk", 8)
+                    task({"S": 225}, [("h", banks[k])] + coefs, [("pk", r)],
+                         affine(pk[r][:], hv(k, d), col[:, 3 + k, t : t + 1], gb[:, c, k, t : t + 1]))
+                    task({"V": 230}, [("a2", r2[d]), ("pk", r)], [("u", c % 2, k, t)],
+                         stt(u_t[c % 2][:, t, k, :], a2[r2[d]][:], ngn[:, k, t : t + 1], pk[r][:]))
+
+        u_codes = sb("u_codes", [C * B], U32, C)
+        u_scales = sb("u_scales", [C * B], U8, C)
+        u_grp = sb("u_grp", [4 * B], BF16, 3)
+
+        def pack_u(c):
+            for k in range(C):
+                r = ring("ug", 3)
+                src_keys = [("u", c % 2, k, t) for t in range(4)]
+                def move(e, k=k, r=r):
+                    copy_on(e, u_grp[r][:].rearrange("p (m t) -> p m t", t=4), u_t[c % 2][:, :, k, :].rearrange("p t m -> p m t"))
+
+                task({"V": 530, "S": 1000}, src_keys, [("ug", r)], move)
+                cols = slice(k * B, (k + 1) * B)
+                task({"V": 240}, [("ug", r)], [("uc", c, k)], quant(u_codes[c][:, cols], u_scales[c][:, cols], u_grp[r][:]))
+
+        raw_y = sb("raw", [V], F32, 2)
+        sums = sb("sums", [2], F32, 3)
+        nmean = sb("nm", [1], F32, 3)
+        cb = sb("cb", [V], BF16, 3)
+        cent = sb("cent", [V], F32, 2)
+        qc = sb("qc", [2, C, 4 * P], BF16, 2)
+
+        def m_tile(c, bh):
+            rr = ring("raw", 2)
+            rb = ring("cb", 3)
+            rc = ring("cent", 2)
+            for vh in range(2):
+                i = ring("y", 2)
+
+                def mm(e, vh=vh, i=i):
+                    for k in range(C):
+                        ucol = k * B + bh * P
+                        scol = k * V + vh * 512
+                        nc.tensor.matmul_mx(
+                            out=y_ps[i][:],
+                            lhsT=u_codes[c][:, ucol : ucol + P].bitcast(FP8X4),
+                            lhsT_scale=u_scales[c][:, ucol : ucol + P],
+                            rhs=s_codes[:, scol : scol + 512].bitcast(FP8X4),
+                            rhs_scale=s_scales[:, scol : scol + 512],
+                            start=(k == 0),
+                            stop=(k == C - 1),
+                        )
+
+                task({"P": 665}, [("uc", c, k) for k in range(C)] + [("sc", 2 * k + vh) for k in range(C)], [("y", i)], mm)
+
+                def evac(e, vh=vh, i=i):
+                    dst = raw_y[rr][:, vh * 512 : (vh + 1) * 512]
+                    acc = sums[rr][:, vh : vh + 1]
+                    if e == "S":
+                        nc.scalar.activation(out=dst, in_=y_ps[i][:], func=ACT.Identity, accum_out=acc)
+                    else:
+                        nc.vector.tensor_scalar(out=dst, in0=y_ps[i][:], scalar1=1.0, scalar2=0.0, op0=ALU.mult, op1=ALU.add, accum_out=acc)
+
+                task({"V": 480, "S": 455}, [("y", i)], [("raw", rr, vh)], evac)
+            both = [("raw", rr, 0), ("raw", rr, 1)]
+            task({"V": 60}, both, [("nm", rr)], lambda e: nc.vector.tensor_scalar(
+                out=nmean[rr][:], in0=sums[rr][:, 0:1], scalar1=sums[rr][:, 1:2], scalar2=-1.0 / V, op0=ALU.add, op1=ALU.mult))
+            task({"V": 440}, both + [("nm", rr)], [("cb", rb)], lambda e: nc.vector.tensor_scalar(
+                out=cb[rb][:], in0=raw_y[rr][:], scalar1=nmean[rr][:], scalar2=None, op0=ALU.add))
+
+            def centre(e):
+                if e == "S":
+                    nc.scalar.activation(out=cent[rc][:], in_=raw_y[rr][:], func=ACT.Identity, bias=nmean[rr][:])
+                elif e == "G":
+                    nc.gpsimd.tensor_scalar(out=cent[rc][:], in0=raw_y[rr][:], scalar1=nmean[rr][:], scalar2=0.0, op0=ALU.add, op1=ALU.add)
+                else:
+                    nc.vector.tensor_scalar(out=cent[rc][:], in0=raw_y[rr][:], scalar1=nmean[rr][:], scalar2=None, op0=ALU.add)
+
+            task({"V": 440, "S": 870}, both + [("nm", rr)], [("cent", rc)], centre)
+            task({"D": 880}, [("cent", rc)], [("out", c, bh)], lambda e: nc.sync.dma_start(
+                out=out[bh * P : (bh + 1) * P, c, :], in_=cent[rc][:]))
+            i = ring("m", 2)
+            tp = m_ps[i][:].rearrange("p (g u m) -> p g u m", g=2, u=2)
+
+            def turn(e):
+                cw = cb[rb][:].bitcast(F32)
+                for gr in range(2):
+                    for u in range(2):
+                        nc.tensor.transpose(tp[:, gr, u, :], cw[:, 256 * gr + u : 256 * (gr + 1) : 2], ident[:])
+
+            task({"P": 550}, [("cb", rb)], [("m", i)], turn)
+
+            def planes_in(e):
+                copy_on(e, qc[bh][:, :, c, :].bitcast(F32).rearrange("p g (m u) -> p g m u", u=2), tp.rearrange("p g u m -> p g m u"))
+
+            task({"V": 440, "S": 435}, [("m", i)], [("qc", bh, c)], planes_in)
+
         words_i = words.bitcast(I32).rearrange("g p m t -> p g (m t)")
         scales_i = scales.bitcast(I32)
-        p_scales = keep.tile([P, 2, C * B], U8, name="p_scales", align_bytes=64)
+        nat = sb("nat", [C * 4 * P], BF16, 2)
+        p_codes = sb("p_codes", [2, C * P], U32, 2)
+        p_scales = sb("p_scales", [2, C * B], U8)
 
-        def m_tile(h, i):
-            raw = ring.tile([P, V], F32, name="raw")
-            sums = ring.tile([P, 2], F32, name="sums")
-            for vh in range(2):
-                y = psum.tile([P, 512], F32, name="y", tag="y", bufs=2)
-                for k in range(C):
-                    ucol = k * HM + i * P
-                    scol = k * V + vh * 512
-                    nc.tensor.matmul_mx(
-                        out=y[:],
-                        lhsT=u_codes[h][:, ucol : ucol + P].bitcast(FP8X4),
-                        lhsT_scale=u_scales[h][:, ucol : ucol + P],
-                        rhs=s_codes[:, scol : scol + 512].bitcast(FP8X4),
-                        rhs_scale=s_scales[:, scol : scol + 512],
-                        start=(k == 0),
-                        stop=(k == C - 1),
-                    )
-                nc.scalar.activation(
-                    out=raw[:, vh * 512 : (vh + 1) * 512], in_=y[:], func=ACT.Identity,
-                    accum_out=sums[:, vh : vh + 1],
-                )
-            nm = ring.tile([P, 1], F32, name="nm")
-            nc.vector.tensor_scalar(
-                out=nm[:], in0=sums[:, 0:1], scalar1=sums[:, 1:2], scalar2=-1.0 / V, op0=ALU.add, op1=ALU.mult
-            )
-            cb = ring.tile([P, V], BF16, name="cb")
-            nc.vector.tensor_scalar(out=cb[:], in0=raw[:], scalar1=nm[:], scalar2=None, op0=ALU.add)
-            cent = ring.tile([P, V], F32, name="cent")
-            nc.vector.tensor_scalar(out=cent[:], in0=raw[:], scalar1=nm[:], scalar2=None, op0=ALU.add)
-            m0 = h * HM + i * P
-            nc.sync.dma_start(out=out_rows[m0 : m0 + P, :], in_=cent[:])
-            tp = psum.tile([P, 2, 2, P], F32, name="tp", tag="mt", bufs=2)
-            cw = cb[:].bitcast(F32)
+        def planes(bh):
+            m0 = bh * C * P
             for gr in range(2):
-                for u in range(2):
-                    nc.tensor.transpose(
-                        tp[:, gr, u, :], cw[:, 256 * gr + u : 256 * (gr + 1) : 2], ident[:]
+                n = nat[gr]
+
+                def mix(e, gr=gr, n=n):
+                    nc.vector.tensor_copy(
+                        out=n[:].rearrange("p (m c t) -> p m c t", c=C, t=4),
+                        in_=qc[bh][:, gr].rearrange("p c (m t) -> p m c t", t=4),
                     )
-            qin = ring.tile([P, 2 * 4 * P], BF16, name="qin", align_bytes=64)
-            nc.scalar.copy(
-                out=qin[:].bitcast(F32).rearrange("p (g m u) -> p g m u", g=2, u=2),
-                in_=tp[:].rearrange("p g u m -> p g m u"),
-            )
-            codes = ring.tile([P, 2, P], U32, name="codes", align_bytes=64)
-            for gr in range(2):
-                nc.vector.quantize_mx(
-                    out=codes[:, gr, :].bitcast(FP8X4),
-                    scales=p_scales[:, gr, m0 : m0 + P],
-                    in_=qin[:, gr * 512 : (gr + 1) * 512],
-                )
-            nc.sync.dma_start(out=words_i[:, :, m0 : m0 + P], in_=codes[:].bitcast(I32))
 
-        def store_scales(h):
-            for q in range(4):
-                nc.sync.dma_start(
-                    out=scales_i[:, 4 * q : 4 * q + 4, h * 96 : (h + 1) * 96].rearrange("g r m -> r g m"),
-                    in_=p_scales[32 * q : 32 * q + 4, :, h * HM : (h + 1) * HM].bitcast(I32),
-                )
+                task({"V": 330}, [("qc", bh, c) for c in range(C)], [("nat", gr)], mix)
+                for lo, width in ((0, 256), (256, 128)):
+                    task({"V": width}, [("nat", gr)], [("pc", bh, gr, lo)],
+                         quant(p_codes[bh][:, gr, lo : lo + width], p_scales[:, gr, m0 + lo : m0 + lo + width], n[:, 4 * lo : 4 * (lo + width)]))
+            keys = [("pc", bh, gr, lo) for gr in range(2) for lo in (0, 256)]
+            task({"D": 700}, keys, [("words", bh)], lambda e: nc.sync.dma_start(
+                out=words_i[:, :, m0 : m0 + C * P], in_=p_codes[bh][:].bitcast(I32)))
 
-        for t in range(4):
-            unit(0, t)
-        for q in range(6):
-            s_piece(q)
-        pack_u(0)
-        for i in range(3):
-            m_tile(0, i)
-        store_scales(0)
-        for t in range(4):
-            unit(1, t)
-        pack_u(1)
-        for i in range(3):
-            m_tile(1, i)
-        store_scales(1)
+            def store_scales(e):
+                for q in range(4):
+                    nc.sync.dma_start(
+                        out=scales_i[:, 4 * q : 4 * q + 4, bh * 96 : (bh + 1) * 96].rearrange("g r m -> r g m"),
+                        in_=p_scales[32 * q : 32 * q + 4, :, m0 : m0 + C * P].bitcast(I32),
+                    )
+
+            task({"D": 300}, keys, [("scales", bh)], store_scales)
+
+        makers = {"W": w_block, "Z": z_all, "V": coef, "S": s_piece, "B": stage1, "K": pack_u, "C": m_tile, "R": planes}
+        for item in ORDER.split(","):
+            parts = item.split()
+            makers[parts[0]](*[int(x) for x in parts[1:]])
+        with tc.manual_schedule():
+            for start, e, i in list_schedule(tasks):
+                costs, reads, writes, emit = tasks[i]
+                if emit is not None:
+                    emit(e)

@@ -17,10 +17,11 @@ B, D, C, F, V = 256, 512, 3, 512, 1024
 E = C * F
 J = C * C * F
 FLOPS = 2 * B * D * J + 2 * B * C * E * V
-LOADS = "w:0:1 v w:1:1 z w:2:1 s:0 s:1 s:2 w:3:3 w:6:3"
-ORDER = "W 0, W 1, W 2, V, Z, B 0 0, B 0 1, K 0, S 0, S 1, S 2, S 3, S 4, S 5, W 3, W 4, W 5, B 1 0, B 1 1, K 1, C 0 0, C 0 1, W 6, W 7, W 8, B 2 0, B 2 1, K 2, C 1 0, C 1 1, C 2 0, R 0, C 2 1, R 1"
+STEPS = "p1 y p2 a1 a2 p0 u1 u2 u0"
+LOADS = "v w:1:2 z s:0 w:0:1 s:1 w:5:1 w:6:1 w:7:2 s:2 w:3:1 w:4:1"
+ORDER = "W 1, V, S 0 V, Z, W 2 S, W 0 H, S 2 V, B 0 2 0 3, S 1 S, W 5 H, S 4 S, W 7 V, W 3 S, B 0 0 0 1, W 6, W 4 S, B 1 2 1 3, W 8 H, B 1 0 1 1, K 0, S 3 V, S 5 S, K 1 V, B 2 0 2 1, B 2 2 2 3, M 0 1, K 2, M 0 0 S, C 1 0 S, C 1 1 S, C 2 0 S, R 0, C 2 1, R 1"
 
-LATENCY = {"V": 70, "S": 70, "P": 110, "D": 1700, "G": 150}
+LATENCY = {"V": 60, "S": 60, "P": 110, "D": 2000, "G": 150}
 
 
 def list_schedule(tasks):
@@ -94,8 +95,12 @@ def tile_neuraljacobianfieldpoissonintegration_x1_kernel(tc, z, w, b, nrm, g, s,
 
         tasks = []
 
+        def either(v, s, only):
+            both = {"V": v, "S": s}
+            return both if only is None else {only: both[only]}
+
         def task(costs, reads, writes, emit):
-            tasks.append((costs, reads, writes, emit))
+            tasks.append(({e: c + (45 if e in "VS" else 0) for e, c in costs.items()}, reads, writes, emit))
 
         turns = {}
 
@@ -119,15 +124,15 @@ def tile_neuraljacobianfieldpoissonintegration_x1_kernel(tc, z, w, b, nrm, g, s,
             for i in range(n):
                 w_raw[b0 + i] = (raw, i, b0)
             nc.sync.dma_start(out=raw[:], in_=w[:, b0 * F : (b0 + n) * F].rearrange("(p j) c -> p j c", j=4))
-            task({"D": n * 880}, [], [("wraw", b0)], None)
+            task({"D": n * (1160 if n == 1 else 1020 if n == 2 else 960)}, [], [("wraw", b0)], None)
 
         def load_s(k):
             nc.sync.dma_start(out=s_raw[k][:], in_=s[k * F : (k + 1) * F, :].rearrange("(p j) v -> p j v", j=4))
-            task({"D": 1760}, [], [("sraw", k)], None)
+            task({"D": 2030}, [], [("sraw", k)], None)
 
         def load_z():
             nc.sync.dma_start(out=z_raw[:], in_=z.rearrange("(r p) k -> p r k", p=P))
-            task({"D": 440}, [], ["zraw"], None)
+            task({"D": 580}, [], ["zraw"], None)
 
         def load_v():
             nc.scalar.dma_start(out=vec[0:3, :], in_=nrm)
@@ -135,7 +140,7 @@ def tile_neuraljacobianfieldpoissonintegration_x1_kernel(tc, z, w, b, nrm, g, s,
             nc.scalar.dma_start(out=vec[6:15, :], in_=b.rearrange("(r f) -> r f", f=F))
             task({"D": 340}, [], ["vec"], None)
 
-        task({"D": 900}, [], ["start"], None)
+        task({"D": 1500}, [], ["start"], None)
         loaders = {"w": load_w, "s": load_s, "z": load_z, "v": load_v}
         for item in LOADS.split():
             parts = item.split(":")
@@ -146,6 +151,8 @@ def tile_neuraljacobianfieldpoissonintegration_x1_kernel(tc, z, w, b, nrm, g, s,
         ss = sb("ss", [4], F32)
         ss2 = sb("ss2", [4], F32)
         root = sb("root", [4], F32)
+        ss3 = sb("ss3", [4], F32)
+        ng = sb("ng", [3, 4], F32)
         rinv = sb("rinv", [4], F32)
         n_c = sb("n_c", [3, 4], F32)
         ngn = sb("ngn", [3, 4], F32)
@@ -172,26 +179,33 @@ def tile_neuraljacobianfieldpoissonintegration_x1_kernel(tc, z, w, b, nrm, g, s,
                 )
 
             task({"V": 80}, [("m", i)], ["col"], v1)
-            task({"V": 70}, ["col"], ["sq"], lambda e: nc.vector.tensor_mul(out=sq[:], in0=nrm_c, in1=nrm_c))
-            task({"V": 70}, ["sq"], ["ss"], lambda e: nc.vector.tensor_add(out=ss[:], in0=sq[:, 0, :], in1=sq[:, 1, :]))
-            task({"V": 70}, ["sq", "ss"], ["ss2"], lambda e: nc.vector.scalar_tensor_tensor(
-                out=ss2[:], in0=ss[:], scalar=1e-6, in1=sq[:, 2, :], op0=ALU.add, op1=ALU.add))
-            task({"S": 80}, ["ss2"], ["root"], lambda e: nc.scalar.activation(out=root[:], in_=ss2[:], func=ACT.Sqrt))
+            def gp(reads, writes, emit):
+                task({"G": 150}, reads, writes, emit)
+
+            def tt(dst, in0, in1, op):
+                return lambda e: nc.gpsimd.tensor_tensor(out=dst, in0=in0, in1=in1, op=op)
+
+            def ts(dst, in0, add, mul):
+                return lambda e: nc.gpsimd.tensor_scalar(out=dst, in0=in0, scalar1=add, scalar2=mul, op0=ALU.add, op1=ALU.mult)
+
+            gp(["col"], ["sq"], tt(sq[:], nrm_c, nrm_c, ALU.mult))
+            gp(["sq"], ["ss"], tt(ss[:], sq[:, 0, :], sq[:, 1, :], ALU.add))
+            gp(["sq", "ss"], ["ss2"], tt(ss2[:], ss[:], sq[:, 2, :], ALU.add))
+            gp(["ss2"], ["ss3"], ts(ss3[:], ss2[:], 1e-6, 1.0))
+            task({"S": 80}, ["ss3"], ["root"], lambda e: nc.scalar.activation(out=root[:], in_=ss3[:], func=ACT.Sqrt))
             task({"V": 80}, ["root"], ["rinv"], lambda e: nc.vector.reciprocal(out=rinv[:], in_=root[:]))
-            task({"V": 70}, ["rinv", "col"], ["n_c"], lambda e: nc.vector.tensor_mul(
-                out=n_c[:], in0=nrm_c, in1=rinv[:].unsqueeze(1).to_broadcast([P, 3, 4])))
-            task({"V": 70}, ["n_c", "col"], ["ngn"], lambda e: nc.vector.scalar_tensor_tensor(
-                out=ngn[:], in0=n_c[:], scalar=-1.0, in1=g_c, op0=ALU.mult, op1=ALU.mult))
+            gp(["rinv", "col"], ["n_c"], tt(n_c[:], nrm_c, rinv[:].unsqueeze(1).to_broadcast([P, 3, 4]), ALU.mult))
+            gp(["n_c", "col"], ["ng"], tt(ng[:], n_c[:], g_c, ALU.mult))
+            gp(["ng"], ["ngn"], ts(ngn[:], ng[:], 0.0, -1.0))
+            b_c = col[:, 6:15, :].rearrange("p (c k) t -> p c (k t)", c=C)
 
-            def products(dst, src, c):
-                return lambda e: nc.vector.tensor_mul(out=dst[:, c], in0=col[:, 6 + 3 * c : 9 + 3 * c, :], in1=src)
+            def over_c(v):
+                return v.rearrange("p k t -> p (k t)").unsqueeze(1).to_broadcast([P, C, 12])
 
-            for c in range(C):
-                task({"V": 70}, ["col"], [("gb", c)], products(gb, g_c, c))
-                task({"V": 70}, ["col", "n_c"], [("nb", c)], products(nb, n_c[:], c))
-            task({"V": 70}, [("nb", 0), ("nb", 1), ("nb", 2)], ["beta0"], lambda e: nc.vector.tensor_add(
-                out=beta0[:], in0=nb[:, :, 0, :], in1=nb[:, :, 1, :]))
-            task({"V": 70}, ["beta0"], ["coef"], lambda e: nc.vector.tensor_add(out=beta[:], in0=beta0[:], in1=nb[:, :, 2, :]))
+            gp(["col"], ["gb"], tt(gb[:].rearrange("p c k t -> p c (k t)"), b_c, over_c(g_c), ALU.mult))
+            gp(["col", "n_c"], ["nb"], tt(nb[:].rearrange("p c k t -> p c (k t)"), b_c, over_c(n_c[:]), ALU.mult))
+            gp(["nb"], ["beta0"], tt(beta0[:], nb[:, :, 0, :], nb[:, :, 1, :], ALU.add))
+            gp(["beta0", "nb"], ["coef"], tt(beta[:], beta0[:], nb[:, :, 2, :], ALU.add))
 
         def copy_on(e, dst, src):
             if e == "S":
@@ -203,26 +217,28 @@ def tile_neuraljacobianfieldpoissonintegration_x1_kernel(tc, z, w, b, nrm, g, s,
 
         w_codes = sb("w_codes", [J], U32)
         w_scales = sb("w_scales", [J], U8)
-        w_grp = sb("w_grp", [4 * F], BF16, 3)
+        w_grp = sb("grp", [4 * F], BF16, 5)
 
         def quant(codes, scale, src):
             return lambda e: nc.vector.quantize_mx(out=codes.bitcast(FP8X4), scales=scale, in_=src)
 
-        def w_block(blk):
+        def w_block(blk, only=None):
             raw, i, b0 = w_raw[blk]
-            r = ring("w", 3)
+            r = ring("grp", 5)
             grp = w_grp[r]
 
-            def half(h):
-                m0 = 64 * h
-                dst = grp[:].rearrange("p (t m j) -> p m t j", t=4, j=4)[:, m0 : m0 + 64]
-                src = raw[:, :, i * F : (i + 1) * F].rearrange("p j (m t) -> p m t j", t=4)[:, m0 : m0 + 64]
-                return lambda e: copy_on(e, dst, src)
-
-            for h in range(2):
-                task({"V": 530, "S": 1000}, [("wraw", b0)], [("wg", r, h)], half(h))
+            dst = grp[:].rearrange("p (t m j) -> p m t j", t=4, j=4)
+            src = raw[:, :, i * F : (i + 1) * F].rearrange("p j (m t) -> p m t j", t=4)
+            if only == "H":
+                for m0, e0 in ((0, "V"), (64, "S")):
+                    task(either(530, 990, e0), [("wraw", b0)], [("wg", r, m0)],
+                         lambda e, m0=m0: copy_on(e, dst[:, m0 : m0 + 64], src[:, m0 : m0 + 64]))
+                ready = [("wg", r, 0), ("wg", r, 64)]
+            else:
+                task(either(1060, 1980, only), [("wraw", b0)], [("wg", r, 0), ("wg", r, 64)], lambda e: copy_on(e, dst, src))
+                ready = [("wg", r, 0), ("wg", r, 64)]
             cols = slice(blk * F, (blk + 1) * F)
-            task({"V": 465}, [("wg", r, 0), ("wg", r, 1)], [("wc", blk)], quant(w_codes[:, cols], w_scales[:, cols], grp[:]))
+            task({"V": 465}, ready, [("wc", blk)], quant(w_codes[:, cols], w_scales[:, cols], grp[:]))
 
         z_codes = sb("z_codes", [B], U32)
         z_scales = sb("z_scales", [B], U8)
@@ -239,36 +255,31 @@ def tile_neuraljacobianfieldpoissonintegration_x1_kernel(tc, z, w, b, nrm, g, s,
                         nc.tensor.transpose(zt[:, u, r * P : (r + 1) * P], zw[:, u : D // 2 : 2], ident[:])
 
             task({"P": 450}, ["zraw"], [("m", i)], turn)
-            task({"V": 440}, [("m", i)], ["zg"], lambda e: nc.vector.tensor_copy(
-                out=z_grp[:].bitcast(F32).rearrange("p (m u) -> p m u", u=2), in_=zt.rearrange("p u m -> p m u")))
+            task({"V": 440, "S": 435}, [("m", i)], ["zg"], lambda e: copy_on(
+                e, z_grp[:].bitcast(F32).rearrange("p (m u) -> p m u", u=2), zt.rearrange("p u m -> p m u")))
             task({"V": 240}, ["zg"], ["zc"], quant(z_codes[:], z_scales[:], z_grp[:]))
 
         s_codes = sb("s_codes", [C * V], U32)
         s_scales = sb("s_scales", [C * V], U8)
-        s_grp = sb("s_grp", [4 * 512], BF16, 3)
+        s_grp = w_grp
 
-        def s_piece(q):
+        def s_piece(q, only=None):
             k, vh = divmod(q, 2)
-            r = ring("s", 3)
+            r = ring("grp", 5)
 
-            def half(h):
-                v0 = 256 * h
-                dst = s_grp[r][:].rearrange("p (c t) -> p c t", t=4)[:, v0 : v0 + 256]
-                src = s_raw[k][:, :, vh * 512 + v0 : vh * 512 + v0 + 256].rearrange("p t c -> p c t")
-                return lambda e: copy_on(e, dst, src)
-
-            for h in range(2):
-                task({"V": 530, "S": 1000}, [("sraw", k)], [("sg", r, h)], half(h))
+            dst = s_grp[r][:].rearrange("p (c i t) -> p c t i", i=4, t=4)
+            src = s_raw[k][:, :, vh * 512 : vh * 512 + 512].rearrange("p t (c i) -> p c t i", i=4)
+            task(either(1060, 1980, only), [("sraw", k)], [("wg", r, 0), ("wg", r, 64)], lambda e: copy_on(e, dst, src))
             cols = slice(q * 512, (q + 1) * 512)
-            task({"V": 465}, [("sg", r, 0), ("sg", r, 1)], [("sc", q)], quant(s_codes[:, cols], s_scales[:, cols], s_grp[r][:]))
+            task({"V": 465}, [("wg", r, 0), ("wg", r, 64)], [("sc", q)], quant(s_codes[:, cols], s_scales[:, cols], s_grp[r][:]))
 
-        u_t = sb("u_t", [4, C, B], BF16, 2)
-        y0 = sb("y0_", [B], F32, 4)
-        a1 = sb("a1_", [B], F32, 4)
-        a2 = sb("a2_", [B], F32, 4)
-        pk = sb("pk_", [B], F32, 8)
+        u_t = [sb("u_t%d_" % n, [4, n * B], BF16, C) for n in (2, 1)]
+        y0 = sb("y0_", [2 * B], F32, 2)
+        a1 = sb("a1_", [2 * B], F32, 2)
+        a2 = sb("a2_", [2 * B], F32, 2)
+        pk = sb("pk_", [2 * B], F32, 6)
 
-        coefs = ["coef", "ngn", ("gb", 0), ("gb", 1), ("gb", 2)]
+        coefs = ["coef", "ngn", "gb"]
 
         def stt(dst, in0, scalar, in1):
             return lambda e: nc.vector.scalar_tensor_tensor(out=dst, in0=in0, scalar=scalar, in1=in1, op0=ALU.mult, op1=ALU.add)
@@ -276,7 +287,8 @@ def tile_neuraljacobianfieldpoissonintegration_x1_kernel(tc, z, w, b, nrm, g, s,
         def affine(dst, src, scale, bias):
             return lambda e: nc.scalar.activation(out=dst, in_=src, func=ACT.Identity, scale=scale, bias=bias)
 
-        def stage1(c, tp):
+        def stage1(c0, t0, c1, t1):
+            pair = ((c0, t0), (c1, t1))
             banks = []
             for k in range(C):
                 i = ring("h", 4)
@@ -284,7 +296,8 @@ def tile_neuraljacobianfieldpoissonintegration_x1_kernel(tc, z, w, b, nrm, g, s,
 
                 def mm(e, k=k, i=i):
                     for d in range(2):
-                        col0 = (c * C + k) * F + (2 * tp + d) * P
+                        c, t = pair[d]
+                        col0 = (c * C + k) * F + t * P
                         nc.tensor.matmul_mx(
                             out=h_ps[i][:, d * B : (d + 1) * B],
                             lhsT=w_codes[:, col0 : col0 + P].bitcast(FP8X4),
@@ -295,56 +308,153 @@ def tile_neuraljacobianfieldpoissonintegration_x1_kernel(tc, z, w, b, nrm, g, s,
                             stop=True,
                         )
 
-                task({"P": 230}, ["zc", ("wc", c * C + k)], [("h", i)], mm)
-            ry, r1, r2 = [[ring(n, 4) for d in range(2)] for n in ("y0", "a1", "a2")]
+                task({"P": 230}, ["zc"] + [("wc", c * C + k) for c in (c0, c1)], [("h", i)], mm)
+            r0, r1, r2 = [ring(n, 2) for n in ("y0", "a1", "a2")]
+            spans = ((0, 2),) if t0 == t1 else ((0, 1), (1, 1))
 
-            def hv(k, d):
-                return h_ps[banks[k]][:, d * B : (d + 1) * B]
+            def part(tile, span):
+                return tile[:, span[0] * B : (span[0] + span[1]) * B]
 
-            for d in range(2):
-                t = 2 * tp + d
-                task({"S": 225}, [("h", banks[0])] + coefs, [("y0", ry[d])],
-                     affine(y0[ry[d]][:], hv(0, d), n_c[:, 0, t : t + 1], beta[:, c, t : t + 1]))
-            for d in range(2):
-                t = 2 * tp + d
-                task({"V": 230}, [("h", banks[1]), ("y0", ry[d])] + coefs, [("a1", r1[d])],
-                     stt(a1[r1[d]][:], hv(1, d), n_c[:, 1, t : t + 1], y0[ry[d]][:]))
-            for d in range(2):
-                t = 2 * tp + d
-                task({"V": 230}, [("h", banks[2]), ("a1", r1[d])], [("a2", r2[d])],
-                     stt(a2[r2[d]][:], hv(2, d), n_c[:, 2, t : t + 1], a1[r1[d]][:]))
-            for k in range(C):
+            def read_y0():
                 for d in range(2):
-                    t = 2 * tp + d
-                    r = ring("pk", 8)
-                    task({"S": 225}, [("h", banks[k])] + coefs, [("pk", r)],
-                         affine(pk[r][:], hv(k, d), col[:, 3 + k, t : t + 1], gb[:, c, k, t : t + 1]))
-                    task({"V": 230}, [("a2", r2[d]), ("pk", r)], [("u", c % 2, k, t)],
-                         stt(u_t[c % 2][:, t, k, :], a2[r2[d]][:], ngn[:, k, t : t + 1], pk[r][:]))
+                    c, t = pair[d]
+                    task({"S": 225}, [("h", banks[0])] + coefs, [("y0", r0, d), ("use", banks[0])],
+                         affine(part(y0[r0], (d, 1)), part(h_ps[banks[0]], (d, 1)), n_c[:, 0, t : t + 1], beta[:, c, t : t + 1]))
+
+            def read_a(k, dst, src, kd, ks):
+                for sp in spans:
+                    t = pair[sp[0]][1]
+                    ds = range(sp[0], sp[0] + sp[1])
+                    task({"V": 12 + 213 * sp[1]}, [("h", banks[k])] + [ks + (d,) for d in ds] + coefs, [kd + (d,) for d in ds] + [("use", banks[k])],
+                         stt(part(dst, sp), part(h_ps[banks[k]], sp), n_c[:, k, t : t + 1], part(src, sp)))
+
+            rp = [ring("pk", 6) for k in range(C)]
+
+            def read_p(k):
+                for d in range(2):
+                    c, t = pair[d]
+                    task({"S": 225}, [("h", banks[k])] + coefs, [("pk", rp[k], d), ("use", banks[k])],
+                         affine(part(pk[rp[k]], (d, 1)), part(h_ps[banks[k]], (d, 1)), col[:, 3 + k, t : t + 1], gb[:, c, k, t : t + 1]))
+
+            def make_u(k):
+                for sp in spans:
+                    ds = range(sp[0], sp[0] + sp[1])
+                    c, t = pair[sp[0]]
+                    dst = u_t[c // 2][k][:, t, (c % 2) * B : (c % 2 + sp[1]) * B]
+                    task({"V": 12 + 213 * sp[1]}, [("a2", r2, d) for d in ds] + [("pk", rp[k], d) for d in ds],
+                         [("u", pair[d][0], k, t) for d in ds],
+                         stt(dst, part(a2[r2], sp), ngn[:, k, t : t + 1], part(pk[rp[k]], sp)))
+
+            first = (1, a1[r1], y0[r0], ("a1", r1), ("y0", r0))
+            second = (2, a2[r2], a1[r1], ("a2", r2), ("a1", r1))
+            for step in STEPS.split():
+                {"y": lambda: read_y0(), "a1": lambda: read_a(*first), "a2": lambda: read_a(*second),
+                 "p0": lambda: read_p(0), "p1": lambda: read_p(1), "p2": lambda: read_p(2),
+                 "u0": lambda: make_u(0), "u1": lambda: make_u(1), "u2": lambda: make_u(2)}[step]()
 
         u_codes = sb("u_codes", [C * B], U32, C)
         u_scales = sb("u_scales", [C * B], U8, C)
         u_grp = sb("u_grp", [4 * B], BF16, 3)
 
-        def pack_u(c):
+        def pack_u(c, only=None):
             for k in range(C):
                 r = ring("ug", 3)
-                src_keys = [("u", c % 2, k, t) for t in range(4)]
+                src_keys = [("u", c, k, t) for t in range(4)]
                 def move(e, k=k, r=r):
-                    copy_on(e, u_grp[r][:].rearrange("p (m t) -> p m t", t=4), u_t[c % 2][:, :, k, :].rearrange("p t m -> p m t"))
+                    copy_on(e, u_grp[r][:].rearrange("p (m i t) -> p m t i", i=4, t=4), u_t[c // 2][k][:, :, (c % 2) * B : (c % 2 + 1) * B].rearrange("p t (m i) -> p m t i", i=4))
 
-                task({"V": 530, "S": 1000}, src_keys, [("ug", r)], move)
+                task(either(530, 1000, only), src_keys, [("ug", r)], move)
+                cols = slice(k * B, (k + 1) * B)
+                task({"V": 240}, [("ug", r)], [("uc", c, k)], quant(u_codes[c][:, cols], u_scales[c][:, cols], u_grp[r][:]))
+
+        def pack_u_tensor(c, only=None):
+            for k in range(C):
+                r = ring("ug", 3)
+                i = ring("m", 2)
+                mv = m_ps[i][:].bitcast(BF16)
+
+                def turn(e, k=k, mv=mv):
+                    for x in range(2):
+                        m0 = (c % 2) * B + x * P
+                        nc.tensor.matmul(
+                            mv[:, x * 512 : (x + 1) * 512].rearrange("p (m t) -> p m t", t=4),
+                            ident_bf[:],
+                            u_t[c // 2][k][:, :, m0 : m0 + P].rearrange("p t m -> p m t"),
+                            start=True,
+                            stop=True,
+                        )
+
+                task({"P": 880}, [("u", c, k, t) for t in range(4)], [("m", i)], turn)
+                task(either(440, 440, only), [("m", i)], [("ug", r)], lambda e, r=r, mv=mv: copy_on(e, u_grp[r][:], mv))
                 cols = slice(k * B, (k + 1) * B)
                 task({"V": 240}, [("ug", r)], [("uc", c, k)], quant(u_codes[c][:, cols], u_scales[c][:, cols], u_grp[r][:]))
 
         raw_y = sb("raw", [V], F32, 2)
         sums = sb("sums", [2], F32, 3)
         nmean = sb("nm", [1], F32, 3)
+        junk = sb("junk", [P], BF16, 2)
         cb = sb("cb", [V], BF16, 3)
         cent = sb("cent", [V], F32, 2)
         qc = sb("qc", [2, C, 4 * P], BF16, 2)
 
-        def m_tile(c, bh):
+        def mean_first(c, bh, only=None):
+            rb = ring("cb", 3)
+            rc = ring("cent", 2)
+            rr = ring("raw", 2)
+            i = ring("m", 2)
+            acc = m_ps[i][:, 0:P]
+            u_keys = [("uc", c, k) for k in range(C)]
+
+            def total(e):
+                for k in range(C):
+                    for x in range(V // P):
+                        ucol = k * B + bh * P
+                        scol = k * V + x * P
+                        nc.tensor.matmul_mx(
+                            out=acc,
+                            lhsT=u_codes[c][:, ucol : ucol + P].bitcast(FP8X4),
+                            lhsT_scale=u_scales[c][:, ucol : ucol + P],
+                            rhs=s_codes[:, scol : scol + P].bitcast(FP8X4),
+                            rhs_scale=s_scales[:, scol : scol + P],
+                            start=(k == 0 and x == 0),
+                            stop=(k == C - 1 and x == V // P - 1),
+                        )
+
+            task({"P": 1500}, u_keys + [("sc", q) for q in range(6)], [("m", i)], total)
+            task({"S": 170}, [("m", i)], [("nm", rr)], lambda e: nc.scalar.activation(
+                out=junk[rr][:], in_=acc, func=ACT.Identity, scale=-1.0 / V, accum_out=nmean[rr][:]))
+            for vh in range(2):
+                i = ring("y", 2)
+
+                def mm(e, vh=vh, i=i):
+                    for k in range(C):
+                        ucol = k * B + bh * P
+                        scol = k * V + vh * 512
+                        nc.tensor.matmul_mx(
+                            out=y_ps[i][:],
+                            lhsT=u_codes[c][:, ucol : ucol + P].bitcast(FP8X4),
+                            lhsT_scale=u_scales[c][:, ucol : ucol + P],
+                            rhs=s_codes[:, scol : scol + 512].bitcast(FP8X4),
+                            rhs_scale=s_scales[:, scol : scol + 512],
+                            start=(k == 0),
+                            stop=(k == C - 1),
+                        )
+
+                task({"P": 665}, u_keys + [("sc", 2 * k + vh) for k in range(C)], [("y", i)], mm)
+
+                def evac(e, vh=vh, i=i):
+                    dst = cent[rc][:, vh * 512 : (vh + 1) * 512]
+                    if e == "S":
+                        nc.scalar.activation(out=dst, in_=y_ps[i][:], func=ACT.Identity, bias=nmean[rr][:])
+                    else:
+                        nc.vector.tensor_scalar(out=dst, in0=y_ps[i][:], scalar1=nmean[rr][:], scalar2=None, op0=ALU.add)
+
+                task(either(440, 435, only), [("y", i), ("nm", rr)], [("cent", rc, vh)], evac)
+            halves = [("cent", rc, 0), ("cent", rc, 1)]
+            task({"V": 440, "S": 870}, halves, [("cb", rb)], lambda e: copy_on(e, cb[rb][:], cent[rc][:]))
+            finish(c, bh, rb, rc, only)
+
+        def m_tile(c, bh, only=None):
             rr = ring("raw", 2)
             rb = ring("cb", 3)
             rc = ring("cent", 2)
@@ -375,7 +485,7 @@ def tile_neuraljacobianfieldpoissonintegration_x1_kernel(tc, z, w, b, nrm, g, s,
                     else:
                         nc.vector.tensor_scalar(out=dst, in0=y_ps[i][:], scalar1=1.0, scalar2=0.0, op0=ALU.mult, op1=ALU.add, accum_out=acc)
 
-                task({"V": 480, "S": 455}, [("y", i)], [("raw", rr, vh)], evac)
+                task(either(480, 455, only), [("y", i)], [("raw", rr, vh)], evac)
             both = [("raw", rr, 0), ("raw", rr, 1)]
             task({"V": 60}, both, [("nm", rr)], lambda e: nc.vector.tensor_scalar(
                 out=nmean[rr][:], in0=sums[rr][:, 0:1], scalar1=sums[rr][:, 1:2], scalar2=-1.0 / V, op0=ALU.add, op1=ALU.mult))
@@ -390,8 +500,11 @@ def tile_neuraljacobianfieldpoissonintegration_x1_kernel(tc, z, w, b, nrm, g, s,
                 else:
                     nc.vector.tensor_scalar(out=cent[rc][:], in0=raw_y[rr][:], scalar1=nmean[rr][:], scalar2=None, op0=ALU.add)
 
-            task({"V": 440, "S": 870}, both + [("nm", rr)], [("cent", rc)], centre)
-            task({"D": 880}, [("cent", rc)], [("out", c, bh)], lambda e: nc.sync.dma_start(
+            task(either(440, 870, "V" if only else None), both + [("nm", rr)], [("cent", rc, 0), ("cent", rc, 1)], centre)
+            finish(c, bh, rb, rc, only)
+
+        def finish(c, bh, rb, rc, only):
+            task({"D": 880}, [("cent", rc, 0), ("cent", rc, 1)], [("out", c, bh)], lambda e: nc.sync.dma_start(
                 out=out[bh * P : (bh + 1) * P, c, :], in_=cent[rc][:]))
             i = ring("m", 2)
             tp = m_ps[i][:].rearrange("p (g u m) -> p g u m", g=2, u=2)
@@ -407,48 +520,47 @@ def tile_neuraljacobianfieldpoissonintegration_x1_kernel(tc, z, w, b, nrm, g, s,
             def planes_in(e):
                 copy_on(e, qc[bh][:, :, c, :].bitcast(F32).rearrange("p g (m u) -> p g m u", u=2), tp.rearrange("p g u m -> p g m u"))
 
-            task({"V": 440, "S": 435}, [("m", i)], [("qc", bh, c)], planes_in)
+            task(either(440, 435, only), [("m", i)], [("qc", bh, c)], planes_in)
 
         words_i = words.bitcast(I32).rearrange("g p m t -> p g (m t)")
         scales_i = scales.bitcast(I32)
-        nat = sb("nat", [C * 4 * P], BF16, 2)
-        p_codes = sb("p_codes", [2, C * P], U32, 2)
-        p_scales = sb("p_scales", [2, C * B], U8)
+        nat = sb("nat", [2, C * 4 * P], BF16)
+        p_codes = sb("p_codes", [2 * C * P], U32, 2)
+        p_scales = sb("p_scales", [2 * C * P], U8, 2)
 
         def planes(bh):
             m0 = bh * C * P
             for gr in range(2):
-                n = nat[gr]
 
-                def mix(e, gr=gr, n=n):
+                def mix(e, gr=gr):
                     nc.vector.tensor_copy(
-                        out=n[:].rearrange("p (m c t) -> p m c t", c=C, t=4),
+                        out=nat[:, gr].rearrange("p (m c t) -> p m c t", c=C, t=4),
                         in_=qc[bh][:, gr].rearrange("p c (m t) -> p m c t", t=4),
                     )
 
                 task({"V": 330}, [("qc", bh, c) for c in range(C)], [("nat", gr)], mix)
-                for lo, width in ((0, 256), (256, 128)):
-                    task({"V": width}, [("nat", gr)], [("pc", bh, gr, lo)],
-                         quant(p_codes[bh][:, gr, lo : lo + width], p_scales[:, gr, m0 + lo : m0 + lo + width], n[:, 4 * lo : 4 * (lo + width)]))
-            keys = [("pc", bh, gr, lo) for gr in range(2) for lo in (0, 256)]
+            flat = nat[:].rearrange("p g x -> p (g x)")
+            for lo, width in ((0, 512), (512, 256)):
+                task({"V": width}, [("nat", 0)] + ([("nat", 1)] if lo + width > C * P else []), [("pc", bh, lo)],
+                     quant(p_codes[bh][:, lo : lo + width], p_scales[bh][:, lo : lo + width], flat[:, 4 * lo : 4 * (lo + width)]))
+            keys = [("pc", bh, lo) for lo in (0, 512)]
             task({"D": 700}, keys, [("words", bh)], lambda e: nc.sync.dma_start(
-                out=words_i[:, :, m0 : m0 + C * P], in_=p_codes[bh][:].bitcast(I32)))
+                out=words_i[:, :, m0 : m0 + C * P], in_=p_codes[bh][:].rearrange("p (g m) -> p g m", g=2).bitcast(I32)))
 
             def store_scales(e):
                 for q in range(4):
                     nc.sync.dma_start(
                         out=scales_i[:, 4 * q : 4 * q + 4, bh * 96 : (bh + 1) * 96].rearrange("g r m -> r g m"),
-                        in_=p_scales[32 * q : 32 * q + 4, :, m0 : m0 + C * P].bitcast(I32),
+                        in_=p_scales[bh][32 * q : 32 * q + 4, :].bitcast(I32).rearrange("r (g m) -> r g m", g=2),
                     )
 
             task({"D": 300}, keys, [("scales", bh)], store_scales)
 
-        makers = {"W": w_block, "Z": z_all, "V": coef, "S": s_piece, "B": stage1, "K": pack_u, "C": m_tile, "R": planes}
+        makers = {"W": w_block, "Z": z_all, "V": coef, "S": s_piece, "B": stage1, "K": pack_u, "Q": pack_u_tensor, "C": m_tile, "M": mean_first, "R": planes}
         for item in ORDER.split(","):
             parts = item.split()
-            makers[parts[0]](*[int(x) for x in parts[1:]])
-        with tc.manual_schedule():
-            for start, e, i in list_schedule(tasks):
-                costs, reads, writes, emit = tasks[i]
-                if emit is not None:
-                    emit(e)
+            makers[parts[0]](*[int(x) if x in "0123456789" else x for x in parts[1:]])
+        for i, e in sorted([(i, e) for start, e, i in list_schedule(tasks)]):
+            costs, reads, writes, emit = tasks[i]
+            if emit is not None:
+                emit(e)

@@ -13,554 +13,399 @@ ACT = mybir.ActivationFunctionType
 ALU = mybir.AluOpType
 
 P = 128
-B, D, C, F, V = 256, 512, 3, 512, 1024
-E = C * F
-J = C * C * F
-FLOPS = 2 * B * D * J + 2 * B * C * E * V
-STEPS = "p1 y p2 a1 a2 p0 u1 u2 u0"
-LOADS = "v w:1:2 z s:0 w:0:1 s:1 w:5:1 w:6:1 w:7:2 s:2 w:3:1 w:4:1"
-ORDER = "W 1, V, S 0 V, Z, W 2 S, W 0 H, S 2 V, B 0 2 0 3, S 1 S, W 5 H, S 4 S, W 7 V, W 3 S, B 0 0 0 1, W 6, W 4 S, B 1 2 1 3, W 8 H, B 1 0 1 1, K 0, S 3 V, S 5 S, K 1 V, B 2 0 2 1, B 2 2 2 3, M 0 1, K 2, M 0 0 S, C 1 0 S, C 1 1 S, C 2 0 S, R 0, C 2 1, R 1"
+PACK = 4
+BATCH, LATENT, COORDS, FACES, VERTS = 256, 512, 3, 512, 1024
+JAC = COORDS * COORDS * FACES
+BANK = 512
+EPS = 1e-6
+FLOPS = 2 * BATCH * LATENT * JAC + 2 * BATCH * COORDS * COORDS * FACES * VERTS
 
-LATENCY = {"V": 60, "S": 60, "P": 110, "D": 2000, "G": 150}
+LOADS = (
+    ("w", 1, 1), ("vectors",), ("w", 2, 1), ("z",), ("s", 0), ("w", 0, 1), ("s", 1), ("w", 5, 1), ("w", 6, 1),
+    ("w", 7, 2), ("s", 2), ("w", 3, 1), ("w", 4, 1),
+)
 
-
-def list_schedule(tasks):
-    writer, readers = {}, {}
-    after = []
-    for i, (costs, reads, writes, emit) in enumerate(tasks):
-        need = set()
-        for r in reads:
-            if r in writer:
-                need.add(writer[r])
-        for r in writes:
-            if r in writer:
-                need.add(writer[r])
-            for j in readers.get(r, []):
-                need.add(j)
-        for r in reads:
-            readers.setdefault(r, []).append(i)
-        for r in writes:
-            writer[r] = i
-            readers[r] = []
-        after.append(need)
-    free = {}
-    for costs, reads, writes, emit in tasks:
-        for e in costs:
-            free[e] = 0
-    done = {}
-    left = list(range(len(tasks)))
-    order = []
-    while left:
-        best = None
-        for i in left:
-            if not all([j in done for j in after[i]]):
-                continue
-            costs = tasks[i][0]
-            for e in costs:
-                ready = free[e]
-                for j in after[i]:
-                    end, by = done[j]
-                    lag = LATENCY[by] + (90 if by == "V" and e == "V" else 0)
-                    if by == e and e in ("P",):
-                        lag = 0
-                    ready = max(ready, end + lag)
-                key = (ready, i, costs[e])
-                if best is None or key < best[0]:
-                    best = (key, i, e)
-        key, i, e = best
-        done[i] = (key[0] + tasks[i][0][e], e)
-        free[e] = key[0] + tasks[i][0][e]
-        left.remove(i)
-        order.append((key[0], e, i))
-    return sorted(order)
+PLAN = (
+    ("coefficients",), ("w", 1, "V"), ("s", 0, "V"), ("z",), ("w", 2, "S"), ("w", 0, "VS"), ("s", 2, "V"),
+    ("stage1", 0, 1), ("s", 1, "S"), ("w", 5, "VS"), ("s", 4, "S"), ("w", 7, "V"), ("w", 3, "S"),
+    ("stage1", 0, 0), ("w", 6, "S"), ("w", 4, "S"), ("stage1", 1, 1), ("w", 8, "VS"), ("stage1", 1, 0),
+    ("u", 0, "VVV"), ("s", 3, "V"), ("s", 5, "S"), ("u", 1, "VVV"), ("stage1", 2, 0), ("stage1", 2, 1),
+    ("tile_tensor_mean", 0, 1), ("u", 2, "SSV"), ("tile_tensor_mean", 0, 0), ("tile_scalar_mean", 1, 0, "V"),
+    ("tile_scalar_mean", 1, 1, "V"), ("tile_scalar_mean", 2, 0, "V"), ("planes", 0),
+    ("tile_scalar_mean", 2, 1, "S"), ("planes", 1),
+)
 
 
 def tile_neuraljacobianfieldpoissonintegration_x1_kernel(tc, z, w, b, nrm, g, s, out, words, scales):
     nc = tc.nc
     with ExitStack() as ctx:
-        keep = ctx.enter_context(tc.tile_pool(name="keep", bufs=1))
+        sbuf = ctx.enter_context(tc.tile_pool(name="sbuf", bufs=1))
         psum = ctx.enter_context(tc.psum_pool(name="psum", bufs=1))
 
-        def bank(name):
-            return psum.tile([P, 512], F32, name=name)
+        def kept(name, shape, dtype):
+            return sbuf.tile([P] + shape, dtype, name=name, align_bytes=64)
 
-        h_ps = [bank("h%d" % i) for i in range(4)]
-        y_ps = [bank("y%d" % i) for i in range(2)]
-        m_ps = [bank("m%d" % i) for i in range(2)]
+        def rotation(tiles):
+            taken = []
 
-        def sb(name, shape, dt, n=None):
-            if n is None:
-                return keep.tile([P] + shape, dt, name=name, align_bytes=64)
-            return [keep.tile([P] + shape, dt, name="%s%d" % (name, i), align_bytes=64) for i in range(n)]
+            def take():
+                taken.append(len(taken))
+                return tiles[taken[-1] % len(tiles)]
 
-        tasks = []
+            return take
 
-        def either(v, s, only):
-            both = {"V": v, "S": s}
-            return both if only is None else {only: both[only]}
+        def rotating(name, shape, dtype, n):
+            return rotation([kept("%s%d" % (name, i), shape, dtype) for i in range(n)])
 
-        def task(costs, reads, writes, emit):
-            tasks.append(({e: c + (45 if e in "VS" else 0) for e, c in costs.items()}, reads, writes, emit))
+        def banks(name, n):
+            return rotation([psum.tile([P, BANK], F32, name="%s%d" % (name, i)) for i in range(n)])
 
-        turns = {}
+        take_h, take_y, take_turn = banks("h", 4), banks("y", 2), banks("turn", 2)
 
-        def ring(name, n):
-            turns[name] = turns.get(name, -1) + 1
-            return turns[name] % n
-
-        ident = sb("ident", [P], F32)
-        ident_bf = sb("ident_bf", [P], BF16)
-        vec = sb("vec", [F], BF16)
-        nc.gpsimd.memset(vec[:], 0.0)
-        make_identity(nc, ident[:])
-        nc.gpsimd.tensor_copy(out=ident_bf[:], in_=ident[:])
-
-        w_raw = {}
-        z_raw = sb("z_raw", [2, D], BF16)
-        s_raw = sb("s_raw", [4, V], BF16, C)
-
-        def load_w(b0, n):
-            raw = sb("w_raw%d" % b0, [4, n * F], BF16)
-            for i in range(n):
-                w_raw[b0 + i] = (raw, i, b0)
-            nc.sync.dma_start(out=raw[:], in_=w[:, b0 * F : (b0 + n) * F].rearrange("(p j) c -> p j c", j=4))
-            task({"D": n * (1160 if n == 1 else 1020 if n == 2 else 960)}, [], [("wraw", b0)], None)
-
-        def load_s(k):
-            nc.sync.dma_start(out=s_raw[k][:], in_=s[k * F : (k + 1) * F, :].rearrange("(p j) v -> p j v", j=4))
-            task({"D": 2030}, [], [("sraw", k)], None)
-
-        def load_z():
-            nc.sync.dma_start(out=z_raw[:], in_=z.rearrange("(r p) k -> p r k", p=P))
-            task({"D": 580}, [], ["zraw"], None)
-
-        def load_v():
-            nc.scalar.dma_start(out=vec[0:3, :], in_=nrm)
-            nc.scalar.dma_start(out=vec[3:6, :], in_=g)
-            nc.scalar.dma_start(out=vec[6:15, :], in_=b.rearrange("(r f) -> r f", f=F))
-            task({"D": 340}, [], ["vec"], None)
-
-        task({"D": 1500}, [], ["start"], None)
-        loaders = {"w": load_w, "s": load_s, "z": load_z, "v": load_v}
-        for item in LOADS.split():
-            parts = item.split(":")
-            loaders[parts[0]](*[int(x) for x in parts[1:]])
-
-        col = sb("col", [15, 4], F32)
-        sq = sb("sq", [3, 4], F32)
-        ss = sb("ss", [4], F32)
-        ss2 = sb("ss2", [4], F32)
-        root = sb("root", [4], F32)
-        ss3 = sb("ss3", [4], F32)
-        ng = sb("ng", [3, 4], F32)
-        rinv = sb("rinv", [4], F32)
-        n_c = sb("n_c", [3, 4], F32)
-        ngn = sb("ngn", [3, 4], F32)
-        gb = sb("gb", [3, 3, 4], F32)
-        nb = sb("nb", [3, 3, 4], F32)
-        beta0 = sb("beta0", [3, 4], F32)
-        beta = sb("beta", [3, 4], F32)
-        nrm_c = col[:, 0:3, :]
-        g_c = col[:, 3:6, :]
-
-        def coef():
-            i = ring("m", 2)
-            ps = m_ps[i][:].bitcast(BF16)
-
-            def turn(e):
-                for t in range(4):
-                    nc.tensor.transpose(ps[:, t * P : (t + 1) * P], vec[:, t:F:4], ident_bf[:])
-
-            task({"P": 420}, ["vec"], [("m", i)], turn)
-
-            def v1(e):
-                nc.vector.tensor_copy(
-                    out=col[:], in_=ps[:, 0 : 4 * P].rearrange("p (t r) -> p t r", t=4)[:, :, 0:15].rearrange("p t r -> p r t")
-                )
-
-            task({"V": 80}, [("m", i)], ["col"], v1)
-            def gp(reads, writes, emit):
-                task({"G": 150}, reads, writes, emit)
-
-            def tt(dst, in0, in1, op):
-                return lambda e: nc.gpsimd.tensor_tensor(out=dst, in0=in0, in1=in1, op=op)
-
-            def ts(dst, in0, add, mul):
-                return lambda e: nc.gpsimd.tensor_scalar(out=dst, in0=in0, scalar1=add, scalar2=mul, op0=ALU.add, op1=ALU.mult)
-
-            gp(["col"], ["sq"], tt(sq[:], nrm_c, nrm_c, ALU.mult))
-            gp(["sq"], ["ss"], tt(ss[:], sq[:, 0, :], sq[:, 1, :], ALU.add))
-            gp(["sq", "ss"], ["ss2"], tt(ss2[:], ss[:], sq[:, 2, :], ALU.add))
-            gp(["ss2"], ["ss3"], ts(ss3[:], ss2[:], 1e-6, 1.0))
-            task({"S": 80}, ["ss3"], ["root"], lambda e: nc.scalar.activation(out=root[:], in_=ss3[:], func=ACT.Sqrt))
-            task({"V": 80}, ["root"], ["rinv"], lambda e: nc.vector.reciprocal(out=rinv[:], in_=root[:]))
-            gp(["rinv", "col"], ["n_c"], tt(n_c[:], nrm_c, rinv[:].unsqueeze(1).to_broadcast([P, 3, 4]), ALU.mult))
-            gp(["n_c", "col"], ["ng"], tt(ng[:], n_c[:], g_c, ALU.mult))
-            gp(["ng"], ["ngn"], ts(ngn[:], ng[:], 0.0, -1.0))
-            b_c = col[:, 6:15, :].rearrange("p (c k) t -> p c (k t)", c=C)
-
-            def over_c(v):
-                return v.rearrange("p k t -> p (k t)").unsqueeze(1).to_broadcast([P, C, 12])
-
-            gp(["col"], ["gb"], tt(gb[:].rearrange("p c k t -> p c (k t)"), b_c, over_c(g_c), ALU.mult))
-            gp(["col", "n_c"], ["nb"], tt(nb[:].rearrange("p c k t -> p c (k t)"), b_c, over_c(n_c[:]), ALU.mult))
-            gp(["nb"], ["beta0"], tt(beta0[:], nb[:, :, 0, :], nb[:, :, 1, :], ALU.add))
-            gp(["beta0", "nb"], ["coef"], tt(beta[:], beta0[:], nb[:, :, 2, :], ALU.add))
-
-        def copy_on(e, dst, src):
-            if e == "S":
+        def copy_on(engine, dst, src):
+            if engine == "S":
                 nc.scalar.copy(out=dst, in_=src)
-            elif e == "G":
-                nc.gpsimd.tensor_copy(out=dst, in_=src)
             else:
                 nc.vector.tensor_copy(out=dst, in_=src)
 
-        w_codes = sb("w_codes", [J], U32)
-        w_scales = sb("w_scales", [J], U8)
-        w_grp = sb("grp", [4 * F], BF16, 5)
+        def quantize(codes, scale_rows, values):
+            nc.vector.quantize_mx(out=codes.bitcast(FP8X4), scales=scale_rows, in_=values)
 
-        def quant(codes, scale, src):
-            return lambda e: nc.vector.quantize_mx(out=codes.bitcast(FP8X4), scales=scale, in_=src)
+        vectors = kept("vectors", [FACES], BF16)
+        nc.vector.memset(vectors[:], 0.0)
+        ident_bf = kept("ident_bf", [P], BF16)
+        ident = kept("ident", [P], F32)
+        make_identity(nc, ident_bf[:])
+        make_identity(nc, ident[:])
 
-        def w_block(blk, only=None):
-            raw, i, b0 = w_raw[blk]
-            r = ring("grp", 5)
-            grp = w_grp[r]
+        w_block_raw = {}
+        s_raw = {}
+        z_raw = kept("z_raw", [2, LATENT], BF16)
 
-            dst = grp[:].rearrange("p (t m j) -> p m t j", t=4, j=4)
-            src = raw[:, :, i * F : (i + 1) * F].rearrange("p j (m t) -> p m t j", t=4)
-            if only == "H":
-                for m0, e0 in ((0, "V"), (64, "S")):
-                    task(either(530, 990, e0), [("wraw", b0)], [("wg", r, m0)],
-                         lambda e, m0=m0: copy_on(e, dst[:, m0 : m0 + 64], src[:, m0 : m0 + 64]))
-                ready = [("wg", r, 0), ("wg", r, 64)]
+        def load_w(first, n):
+            raw = kept("w_raw%d" % first, [PACK, n * FACES], BF16)
+            cols = w[:, first * FACES : (first + n) * FACES]
+            nc.sync.dma_start(out=raw[:], in_=cols.rearrange("(p t) j -> p t j", t=PACK))
+            for i in range(n):
+                w_block_raw[first + i] = raw[:, :, i * FACES : (i + 1) * FACES]
+
+        def load_s(k):
+            s_raw[k] = kept("s_raw%d" % k, [PACK, VERTS], BF16)
+            rows = s[k * FACES : (k + 1) * FACES, :]
+            nc.sync.dma_start(out=s_raw[k][:], in_=rows.rearrange("(p t) v -> p t v", t=PACK))
+
+        def load_z():
+            nc.sync.dma_start(out=z_raw[:], in_=z.rearrange("(r p) d -> p r d", p=P))
+
+        def load_vectors():
+            nc.sync.dma_start(out=vectors[0:3, :], in_=nrm)
+            nc.sync.dma_start(out=vectors[3:6, :], in_=g)
+            nc.sync.dma_start(out=vectors[6:15, :], in_=b.rearrange("(r f) -> r f", f=FACES))
+
+        loaders = {"w": load_w, "s": load_s, "z": load_z, "vectors": load_vectors}
+        for load in LOADS:
+            loaders[load[0]](*load[1:])
+
+        face = kept("face", [15, PACK], F32)
+        normal_in, gain = face[:, 0:3, :], face[:, 3:6, :]
+        minus_half = kept("minus_half", [PACK], F32)
+        nc.gpsimd.memset(minus_half[:], -0.5)
+        normal = kept("normal", [COORDS, PACK], F32)
+        minus_gn = kept("minus_gn", [COORDS, PACK], F32)
+        gain_bias = kept("gain_bias", [COORDS, COORDS, PACK], F32)
+        normal_bias = kept("normal_bias", [COORDS, PACK], F32)
+
+        def coefficients():
+            turned_vectors = take_turn()[:].bitcast(BF16)
+            for t in range(PACK):
+                nc.tensor.transpose(turned_vectors[:, t * P : (t + 1) * P], vectors[:, t:FACES:PACK], ident_bf[:])
+            by_t = turned_vectors[:, 0 : PACK * P].rearrange("p (t r) -> p t r", t=PACK)
+            nc.vector.tensor_copy(out=face[:], in_=by_t[:, :, 0:15].rearrange("p t r -> p r t"))
+
+            def combine(dst, in0, in1, op):
+                nc.gpsimd.tensor_tensor(out=dst, in0=in0, in1=in1, op=op)
+
+            square = kept("square", [COORDS, PACK], F32)
+            two = kept("two", [PACK], F32)
+            three = kept("three", [PACK], F32)
+            shifted = kept("shifted", [PACK], F32)
+            inverse = kept("inverse", [PACK], F32)
+            gn = kept("gn", [COORDS, PACK], F32)
+            nb = kept("nb", [COORDS, COORDS, PACK], F32)
+            nb_two = kept("nb_two", [COORDS, PACK], F32)
+
+            combine(square[:], normal_in, normal_in, ALU.mult)
+            combine(two[:], square[:, 0, :], square[:, 1, :], ALU.add)
+            combine(three[:], two[:], square[:, 2, :], ALU.add)
+            nc.gpsimd.tensor_scalar(
+                out=shifted[:], in0=three[:], scalar1=EPS, scalar2=1.0, op0=ALU.add, op1=ALU.mult
+            )
+            combine(inverse[:], shifted[:], minus_half[:], ALU.pow)
+            combine(normal[:], normal_in, inverse[:].unsqueeze(1).to_broadcast([P, COORDS, PACK]), ALU.mult)
+            combine(gn[:], normal[:], gain, ALU.mult)
+            nc.gpsimd.tensor_scalar(
+                out=minus_gn[:], in0=gn[:], scalar1=0.0, scalar2=-1.0, op0=ALU.add, op1=ALU.mult
+            )
+            bias = face[:, 6:15, :].rearrange("p (c k) t -> p c (k t)", c=COORDS)
+
+            def for_each_c(per_k):
+                return per_k.rearrange("p k t -> p (k t)").unsqueeze(1).to_broadcast([P, COORDS, COORDS * PACK])
+
+            combine(gain_bias[:].rearrange("p c k t -> p c (k t)"), bias, for_each_c(gain), ALU.mult)
+            combine(nb[:].rearrange("p c k t -> p c (k t)"), bias, for_each_c(normal[:]), ALU.mult)
+            combine(nb_two[:], nb[:, :, 0, :], nb[:, :, 1, :], ALU.add)
+            combine(normal_bias[:], nb_two[:], nb[:, :, 2, :], ALU.add)
+
+        w_codes = kept("w_codes", [JAC], U32)
+        w_scales = kept("w_scales", [JAC], U8)
+
+        take_grouped = rotating("grouped", [PACK * FACES], BF16, 5)
+
+        def quantize_w(block, engines):
+            grouped = take_grouped()
+            dst = grouped[:].rearrange("p (t m j) -> p m t j", t=PACK, j=PACK)
+            src = w_block_raw[block].rearrange("p j (m t) -> p m t j", t=PACK)
+            share = P // len(engines)
+            for i, engine in enumerate(engines):
+                part = slice(i * share, (i + 1) * share)
+                copy_on(engine, dst[:, part], src[:, part])
+            cols = slice(block * FACES, (block + 1) * FACES)
+            quantize(w_codes[:, cols], w_scales[:, cols], grouped[:])
+
+        z_codes = kept("z_codes", [BATCH], U32)
+        z_scales = kept("z_scales", [BATCH], U8)
+
+        def quantize_z():
+            pairs = take_turn()[:].rearrange("p (u i) -> p u i", u=2)
+            for r in range(2):
+                rows = z_raw[:, r, :].bitcast(F32)
+                for u in range(2):
+                    nc.tensor.transpose(pairs[:, u, r * P : (r + 1) * P], rows[:, u : LATENT // 2 : 2], ident[:])
+            grouped = kept("z_grouped", [PACK * BATCH], BF16)
+            nc.vector.tensor_copy(
+                out=grouped[:].bitcast(F32).rearrange("p (i u) -> p i u", u=2), in_=pairs.rearrange("p u i -> p i u")
+            )
+            quantize(z_codes[:], z_scales[:], grouped[:])
+
+        s_codes = kept("s_codes", [COORDS * VERTS], U32)
+        s_scales = kept("s_scales", [COORDS * VERTS], U8)
+
+        def interleave(engine, dst, src):
+            copy_on(
+                engine, dst.rearrange("p (x i t) -> p x t i", i=4, t=PACK), src.rearrange("p t (x i) -> p x t i", i=4)
+            )
+
+        def quantize_s(half, engine):
+            k, v_half = divmod(half, 2)
+            grouped = take_grouped()
+            interleave(engine, grouped[:], s_raw[k][:, :, v_half * BANK : (v_half + 1) * BANK])
+            cols = slice(half * BANK, (half + 1) * BANK)
+            quantize(s_codes[:, cols], s_scales[:, cols], grouped[:])
+
+        u_first = [kept("u_first%d" % k, [PACK, 2 * BATCH], BF16) for k in range(COORDS)]
+        u_last = [kept("u_last%d" % k, [PACK, BATCH], BF16) for k in range(COORDS)]
+
+        def u_of(c, k):
+            return u_last[k][:] if c == 2 else u_first[k][:, :, c * BATCH : (c + 1) * BATCH]
+
+        take_along0 = rotating("along0_", [2 * BATCH], F32, 2)
+        take_along01 = rotating("along01_", [2 * BATCH], F32, 2)
+        take_along = rotating("along", [2 * BATCH], F32, 2)
+        take_scaled = rotating("scaled", [2 * BATCH], F32, 6)
+
+        def halves(tile):
+            return [tile[:, i * BATCH : (i + 1) * BATCH] for i in range(2)]
+
+        def stage1(c, pair):
+            slices = (2 * pair, 2 * pair + 1)
+            h = []
+            for k in range(COORDS):
+                h_k = take_h()
+                for i, t in enumerate(slices):
+                    col = (c * COORDS + k) * FACES + t * P
+                    nc.tensor.matmul_mx(
+                        out=h_k[:, i * BATCH : (i + 1) * BATCH],
+                        lhsT=w_codes[:, col : col + P].bitcast(FP8X4),
+                        lhsT_scale=w_scales[:, col : col + P],
+                        rhs=z_codes[:].bitcast(FP8X4),
+                        rhs_scale=z_scales[:],
+                        start=True,
+                        stop=True,
+                    )
+                h.append(halves(h_k))
+
+            along0, along01, along = halves(take_along0()), halves(take_along01()), halves(take_along())
+            scaled = [halves(take_scaled()) for k in range(COORDS)]
+
+            def scale_h(k):
+                for i, t in enumerate(slices):
+                    nc.scalar.activation(
+                        out=scaled[k][i], in_=h[k][i], func=ACT.Identity,
+                        scale=face[:, 3 + k, t : t + 1], bias=gain_bias[:, c, k, t : t + 1],
+                    )
+
+            def multiply_add(dst, in0, per_face, in1):
+                nc.vector.scalar_tensor_tensor(
+                    out=dst, in0=in0, scalar=per_face, in1=in1, op0=ALU.mult, op1=ALU.add
+                )
+
+            scale_h(1)
+            for i, t in enumerate(slices):
+                nc.scalar.activation(
+                    out=along0[i], in_=h[0][i], func=ACT.Identity,
+                    scale=normal[:, 0, t : t + 1], bias=normal_bias[:, c, t : t + 1],
+                )
+            scale_h(2)
+            for i, t in enumerate(slices):
+                multiply_add(along01[i], h[1][i], normal[:, 1, t : t + 1], along0[i])
+            for i, t in enumerate(slices):
+                multiply_add(along[i], h[2][i], normal[:, 2, t : t + 1], along01[i])
+            scale_h(0)
+            for k in (1, 2, 0):
+                for i, t in enumerate(slices):
+                    multiply_add(u_of(c, k)[:, t, :], along[i], minus_gn[:, k, t : t + 1], scaled[k][i])
+
+        u_codes = [kept("u_codes%d" % c, [COORDS * BATCH], U32) for c in range(COORDS)]
+        u_scales = [kept("u_scales%d" % c, [COORDS * BATCH], U8) for c in range(COORDS)]
+
+        take_u_grouped = rotating("u_grouped", [PACK * BATCH], BF16, 3)
+
+        def quantize_u(c, engines):
+            for k in range(COORDS):
+                grouped = take_u_grouped()
+                interleave(engines[k], grouped[:], u_of(c, k))
+                cols = slice(k * BATCH, (k + 1) * BATCH)
+                quantize(u_codes[c][:, cols], u_scales[c][:, cols], grouped[:])
+
+        for_planes = [kept("for_planes%d" % b_half, [2, COORDS, PACK * P], BF16) for b_half in range(2)]
+
+        take_rounded = rotating("rounded", [VERTS], BF16, 3)
+        take_centred = rotating("centred", [VERTS], F32, 2)
+        take_raw = rotating("raw", [VERTS], F32, 2)
+        take_sums = rotating("sums", [2], F32, 2)
+        take_minus_mean = rotating("minus_mean", [1], F32, 2)
+        take_written = rotating("written", [P], BF16, 2)
+
+        def pass_over(dst, c, b_half, k, v, n, start, stop):
+            row = k * BATCH + b_half * P
+            col = k * VERTS + v
+            nc.tensor.matmul_mx(
+                out=dst,
+                lhsT=u_codes[c][:, row : row + P].bitcast(FP8X4),
+                lhsT_scale=u_scales[c][:, row : row + P],
+                rhs=s_codes[:, col : col + n].bitcast(FP8X4),
+                rhs_scale=s_scales[:, col : col + n],
+                start=start,
+                stop=stop,
+            )
+
+        def product(c, b_half, v_half):
+            y = take_y()
+            for k in range(COORDS):
+                pass_over(y[:], c, b_half, k, v_half * BANK, BANK, k == 0, k == COORDS - 1)
+            return y
+
+        def tile_tensor_mean(c, b_half):
+            rounded = take_rounded()
+            centred = take_centred()
+            minus_mean = take_minus_mean()
+            folded = take_turn()
+            for k in range(COORDS):
+                for v in range(0, VERTS, P):
+                    pass_over(
+                        folded[:, 0:P], c, b_half, k, v, P,
+                        k == 0 and v == 0, k == COORDS - 1 and v == VERTS - P,
+                    )
+            written = take_written()
+            nc.scalar.activation(
+                out=written[:], in_=folded[:, 0:P], func=ACT.Identity, scale=-1.0 / VERTS, accum_out=minus_mean[:]
+            )
+            for v_half in range(2):
+                y = product(c, b_half, v_half)
+                nc.scalar.activation(
+                    out=centred[:, v_half * BANK : (v_half + 1) * BANK], in_=y[:], func=ACT.Identity, bias=minus_mean[:]
+                )
+            nc.scalar.copy(out=rounded[:], in_=centred[:])
+            finish(c, b_half, rounded, centred)
+
+        def tile_scalar_mean(c, b_half, engine):
+            raw = take_raw()
+            rounded = take_rounded()
+            centred = take_centred()
+            sums = take_sums()
+            minus_mean = take_minus_mean()
+            for v_half in range(2):
+                y = product(c, b_half, v_half)
+                nc.scalar.activation(
+                    out=raw[:, v_half * BANK : (v_half + 1) * BANK], in_=y[:], func=ACT.Identity,
+                    accum_out=sums[:, v_half : v_half + 1],
+                )
+            nc.vector.tensor_scalar(
+                out=minus_mean[:], in0=sums[:, 0:1], scalar1=sums[:, 1:2], scalar2=-1.0 / VERTS,
+                op0=ALU.add, op1=ALU.mult,
+            )
+            nc.vector.tensor_scalar(out=rounded[:], in0=raw[:], scalar1=minus_mean[:], scalar2=None, op0=ALU.add)
+            if engine == "S":
+                nc.scalar.activation(out=centred[:], in_=raw[:], func=ACT.Identity, bias=minus_mean[:])
             else:
-                task(either(1060, 1980, only), [("wraw", b0)], [("wg", r, 0), ("wg", r, 64)], lambda e: copy_on(e, dst, src))
-                ready = [("wg", r, 0), ("wg", r, 64)]
-            cols = slice(blk * F, (blk + 1) * F)
-            task({"V": 465}, ready, [("wc", blk)], quant(w_codes[:, cols], w_scales[:, cols], grp[:]))
+                nc.vector.tensor_scalar(out=centred[:], in0=raw[:], scalar1=minus_mean[:], scalar2=None, op0=ALU.add)
+            finish(c, b_half, rounded, centred)
 
-        z_codes = sb("z_codes", [B], U32)
-        z_scales = sb("z_scales", [B], U8)
-        z_grp = sb("z_grp", [4 * B], BF16)
-
-        def z_all():
-            i = ring("m", 2)
-            zt = m_ps[i][:].rearrange("p (u m) -> p u m", u=2)
-
-            def turn(e):
-                for r in range(2):
-                    zw = z_raw[:, r, :].bitcast(F32)
-                    for u in range(2):
-                        nc.tensor.transpose(zt[:, u, r * P : (r + 1) * P], zw[:, u : D // 2 : 2], ident[:])
-
-            task({"P": 450}, ["zraw"], [("m", i)], turn)
-            task({"V": 440, "S": 435}, [("m", i)], ["zg"], lambda e: copy_on(
-                e, z_grp[:].bitcast(F32).rearrange("p (m u) -> p m u", u=2), zt.rearrange("p u m -> p m u")))
-            task({"V": 240}, ["zg"], ["zc"], quant(z_codes[:], z_scales[:], z_grp[:]))
-
-        s_codes = sb("s_codes", [C * V], U32)
-        s_scales = sb("s_scales", [C * V], U8)
-        s_grp = w_grp
-
-        def s_piece(q, only=None):
-            k, vh = divmod(q, 2)
-            r = ring("grp", 5)
-
-            dst = s_grp[r][:].rearrange("p (c i t) -> p c t i", i=4, t=4)
-            src = s_raw[k][:, :, vh * 512 : vh * 512 + 512].rearrange("p t (c i) -> p c t i", i=4)
-            task(either(1060, 1980, only), [("sraw", k)], [("wg", r, 0), ("wg", r, 64)], lambda e: copy_on(e, dst, src))
-            cols = slice(q * 512, (q + 1) * 512)
-            task({"V": 465}, [("wg", r, 0), ("wg", r, 64)], [("sc", q)], quant(s_codes[:, cols], s_scales[:, cols], s_grp[r][:]))
-
-        u_t = [sb("u_t%d_" % n, [4, n * B], BF16, C) for n in (2, 1)]
-        y0 = sb("y0_", [2 * B], F32, 2)
-        a1 = sb("a1_", [2 * B], F32, 2)
-        a2 = sb("a2_", [2 * B], F32, 2)
-        pk = sb("pk_", [2 * B], F32, 6)
-
-        coefs = ["coef", "ngn", "gb"]
-
-        def stt(dst, in0, scalar, in1):
-            return lambda e: nc.vector.scalar_tensor_tensor(out=dst, in0=in0, scalar=scalar, in1=in1, op0=ALU.mult, op1=ALU.add)
-
-        def affine(dst, src, scale, bias):
-            return lambda e: nc.scalar.activation(out=dst, in_=src, func=ACT.Identity, scale=scale, bias=bias)
-
-        def stage1(c0, t0, c1, t1):
-            pair = ((c0, t0), (c1, t1))
-            banks = []
-            for k in range(C):
-                i = ring("h", 4)
-                banks.append(i)
-
-                def mm(e, k=k, i=i):
-                    for d in range(2):
-                        c, t = pair[d]
-                        col0 = (c * C + k) * F + t * P
-                        nc.tensor.matmul_mx(
-                            out=h_ps[i][:, d * B : (d + 1) * B],
-                            lhsT=w_codes[:, col0 : col0 + P].bitcast(FP8X4),
-                            lhsT_scale=w_scales[:, col0 : col0 + P],
-                            rhs=z_codes[:].bitcast(FP8X4),
-                            rhs_scale=z_scales[:],
-                            start=True,
-                            stop=True,
-                        )
-
-                task({"P": 230}, ["zc"] + [("wc", c * C + k) for c in (c0, c1)], [("h", i)], mm)
-            r0, r1, r2 = [ring(n, 2) for n in ("y0", "a1", "a2")]
-            spans = ((0, 2),) if t0 == t1 else ((0, 1), (1, 1))
-
-            def part(tile, span):
-                return tile[:, span[0] * B : (span[0] + span[1]) * B]
-
-            def read_y0():
-                for d in range(2):
-                    c, t = pair[d]
-                    task({"S": 225}, [("h", banks[0])] + coefs, [("y0", r0, d), ("use", banks[0])],
-                         affine(part(y0[r0], (d, 1)), part(h_ps[banks[0]], (d, 1)), n_c[:, 0, t : t + 1], beta[:, c, t : t + 1]))
-
-            def read_a(k, dst, src, kd, ks):
-                for sp in spans:
-                    t = pair[sp[0]][1]
-                    ds = range(sp[0], sp[0] + sp[1])
-                    task({"V": 12 + 213 * sp[1]}, [("h", banks[k])] + [ks + (d,) for d in ds] + coefs, [kd + (d,) for d in ds] + [("use", banks[k])],
-                         stt(part(dst, sp), part(h_ps[banks[k]], sp), n_c[:, k, t : t + 1], part(src, sp)))
-
-            rp = [ring("pk", 6) for k in range(C)]
-
-            def read_p(k):
-                for d in range(2):
-                    c, t = pair[d]
-                    task({"S": 225}, [("h", banks[k])] + coefs, [("pk", rp[k], d), ("use", banks[k])],
-                         affine(part(pk[rp[k]], (d, 1)), part(h_ps[banks[k]], (d, 1)), col[:, 3 + k, t : t + 1], gb[:, c, k, t : t + 1]))
-
-            def make_u(k):
-                for sp in spans:
-                    ds = range(sp[0], sp[0] + sp[1])
-                    c, t = pair[sp[0]]
-                    dst = u_t[c // 2][k][:, t, (c % 2) * B : (c % 2 + sp[1]) * B]
-                    task({"V": 12 + 213 * sp[1]}, [("a2", r2, d) for d in ds] + [("pk", rp[k], d) for d in ds],
-                         [("u", pair[d][0], k, t) for d in ds],
-                         stt(dst, part(a2[r2], sp), ngn[:, k, t : t + 1], part(pk[rp[k]], sp)))
-
-            first = (1, a1[r1], y0[r0], ("a1", r1), ("y0", r0))
-            second = (2, a2[r2], a1[r1], ("a2", r2), ("a1", r1))
-            for step in STEPS.split():
-                {"y": lambda: read_y0(), "a1": lambda: read_a(*first), "a2": lambda: read_a(*second),
-                 "p0": lambda: read_p(0), "p1": lambda: read_p(1), "p2": lambda: read_p(2),
-                 "u0": lambda: make_u(0), "u1": lambda: make_u(1), "u2": lambda: make_u(2)}[step]()
-
-        u_codes = sb("u_codes", [C * B], U32, C)
-        u_scales = sb("u_scales", [C * B], U8, C)
-        u_grp = sb("u_grp", [4 * B], BF16, 3)
-
-        def pack_u(c, only=None):
-            for k in range(C):
-                r = ring("ug", 3)
-                src_keys = [("u", c, k, t) for t in range(4)]
-                def move(e, k=k, r=r):
-                    copy_on(e, u_grp[r][:].rearrange("p (m i t) -> p m t i", i=4, t=4), u_t[c // 2][k][:, :, (c % 2) * B : (c % 2 + 1) * B].rearrange("p t (m i) -> p m t i", i=4))
-
-                task(either(530, 1000, only), src_keys, [("ug", r)], move)
-                cols = slice(k * B, (k + 1) * B)
-                task({"V": 240}, [("ug", r)], [("uc", c, k)], quant(u_codes[c][:, cols], u_scales[c][:, cols], u_grp[r][:]))
-
-        def pack_u_tensor(c, only=None):
-            for k in range(C):
-                r = ring("ug", 3)
-                i = ring("m", 2)
-                mv = m_ps[i][:].bitcast(BF16)
-
-                def turn(e, k=k, mv=mv):
-                    for x in range(2):
-                        m0 = (c % 2) * B + x * P
-                        nc.tensor.matmul(
-                            mv[:, x * 512 : (x + 1) * 512].rearrange("p (m t) -> p m t", t=4),
-                            ident_bf[:],
-                            u_t[c // 2][k][:, :, m0 : m0 + P].rearrange("p t m -> p m t"),
-                            start=True,
-                            stop=True,
-                        )
-
-                task({"P": 880}, [("u", c, k, t) for t in range(4)], [("m", i)], turn)
-                task(either(440, 440, only), [("m", i)], [("ug", r)], lambda e, r=r, mv=mv: copy_on(e, u_grp[r][:], mv))
-                cols = slice(k * B, (k + 1) * B)
-                task({"V": 240}, [("ug", r)], [("uc", c, k)], quant(u_codes[c][:, cols], u_scales[c][:, cols], u_grp[r][:]))
-
-        raw_y = sb("raw", [V], F32, 2)
-        sums = sb("sums", [2], F32, 3)
-        nmean = sb("nm", [1], F32, 3)
-        junk = sb("junk", [P], BF16, 2)
-        cb = sb("cb", [V], BF16, 3)
-        cent = sb("cent", [V], F32, 2)
-        qc = sb("qc", [2, C, 4 * P], BF16, 2)
-
-        def mean_first(c, bh, only=None):
-            rb = ring("cb", 3)
-            rc = ring("cent", 2)
-            rr = ring("raw", 2)
-            i = ring("m", 2)
-            acc = m_ps[i][:, 0:P]
-            u_keys = [("uc", c, k) for k in range(C)]
-
-            def total(e):
-                for k in range(C):
-                    for x in range(V // P):
-                        ucol = k * B + bh * P
-                        scol = k * V + x * P
-                        nc.tensor.matmul_mx(
-                            out=acc,
-                            lhsT=u_codes[c][:, ucol : ucol + P].bitcast(FP8X4),
-                            lhsT_scale=u_scales[c][:, ucol : ucol + P],
-                            rhs=s_codes[:, scol : scol + P].bitcast(FP8X4),
-                            rhs_scale=s_scales[:, scol : scol + P],
-                            start=(k == 0 and x == 0),
-                            stop=(k == C - 1 and x == V // P - 1),
-                        )
-
-            task({"P": 1500}, u_keys + [("sc", q) for q in range(6)], [("m", i)], total)
-            task({"S": 170}, [("m", i)], [("nm", rr)], lambda e: nc.scalar.activation(
-                out=junk[rr][:], in_=acc, func=ACT.Identity, scale=-1.0 / V, accum_out=nmean[rr][:]))
-            for vh in range(2):
-                i = ring("y", 2)
-
-                def mm(e, vh=vh, i=i):
-                    for k in range(C):
-                        ucol = k * B + bh * P
-                        scol = k * V + vh * 512
-                        nc.tensor.matmul_mx(
-                            out=y_ps[i][:],
-                            lhsT=u_codes[c][:, ucol : ucol + P].bitcast(FP8X4),
-                            lhsT_scale=u_scales[c][:, ucol : ucol + P],
-                            rhs=s_codes[:, scol : scol + 512].bitcast(FP8X4),
-                            rhs_scale=s_scales[:, scol : scol + 512],
-                            start=(k == 0),
-                            stop=(k == C - 1),
-                        )
-
-                task({"P": 665}, u_keys + [("sc", 2 * k + vh) for k in range(C)], [("y", i)], mm)
-
-                def evac(e, vh=vh, i=i):
-                    dst = cent[rc][:, vh * 512 : (vh + 1) * 512]
-                    if e == "S":
-                        nc.scalar.activation(out=dst, in_=y_ps[i][:], func=ACT.Identity, bias=nmean[rr][:])
-                    else:
-                        nc.vector.tensor_scalar(out=dst, in0=y_ps[i][:], scalar1=nmean[rr][:], scalar2=None, op0=ALU.add)
-
-                task(either(440, 435, only), [("y", i), ("nm", rr)], [("cent", rc, vh)], evac)
-            halves = [("cent", rc, 0), ("cent", rc, 1)]
-            task({"V": 440, "S": 870}, halves, [("cb", rb)], lambda e: copy_on(e, cb[rb][:], cent[rc][:]))
-            finish(c, bh, rb, rc, only)
-
-        def m_tile(c, bh, only=None):
-            rr = ring("raw", 2)
-            rb = ring("cb", 3)
-            rc = ring("cent", 2)
-            for vh in range(2):
-                i = ring("y", 2)
-
-                def mm(e, vh=vh, i=i):
-                    for k in range(C):
-                        ucol = k * B + bh * P
-                        scol = k * V + vh * 512
-                        nc.tensor.matmul_mx(
-                            out=y_ps[i][:],
-                            lhsT=u_codes[c][:, ucol : ucol + P].bitcast(FP8X4),
-                            lhsT_scale=u_scales[c][:, ucol : ucol + P],
-                            rhs=s_codes[:, scol : scol + 512].bitcast(FP8X4),
-                            rhs_scale=s_scales[:, scol : scol + 512],
-                            start=(k == 0),
-                            stop=(k == C - 1),
-                        )
-
-                task({"P": 665}, [("uc", c, k) for k in range(C)] + [("sc", 2 * k + vh) for k in range(C)], [("y", i)], mm)
-
-                def evac(e, vh=vh, i=i):
-                    dst = raw_y[rr][:, vh * 512 : (vh + 1) * 512]
-                    acc = sums[rr][:, vh : vh + 1]
-                    if e == "S":
-                        nc.scalar.activation(out=dst, in_=y_ps[i][:], func=ACT.Identity, accum_out=acc)
-                    else:
-                        nc.vector.tensor_scalar(out=dst, in0=y_ps[i][:], scalar1=1.0, scalar2=0.0, op0=ALU.mult, op1=ALU.add, accum_out=acc)
-
-                task(either(480, 455, only), [("y", i)], [("raw", rr, vh)], evac)
-            both = [("raw", rr, 0), ("raw", rr, 1)]
-            task({"V": 60}, both, [("nm", rr)], lambda e: nc.vector.tensor_scalar(
-                out=nmean[rr][:], in0=sums[rr][:, 0:1], scalar1=sums[rr][:, 1:2], scalar2=-1.0 / V, op0=ALU.add, op1=ALU.mult))
-            task({"V": 440}, both + [("nm", rr)], [("cb", rb)], lambda e: nc.vector.tensor_scalar(
-                out=cb[rb][:], in0=raw_y[rr][:], scalar1=nmean[rr][:], scalar2=None, op0=ALU.add))
-
-            def centre(e):
-                if e == "S":
-                    nc.scalar.activation(out=cent[rc][:], in_=raw_y[rr][:], func=ACT.Identity, bias=nmean[rr][:])
-                elif e == "G":
-                    nc.gpsimd.tensor_scalar(out=cent[rc][:], in0=raw_y[rr][:], scalar1=nmean[rr][:], scalar2=0.0, op0=ALU.add, op1=ALU.add)
-                else:
-                    nc.vector.tensor_scalar(out=cent[rc][:], in0=raw_y[rr][:], scalar1=nmean[rr][:], scalar2=None, op0=ALU.add)
-
-            task(either(440, 870, "V" if only else None), both + [("nm", rr)], [("cent", rc, 0), ("cent", rc, 1)], centre)
-            finish(c, bh, rb, rc, only)
-
-        def finish(c, bh, rb, rc, only):
-            task({"D": 880}, [("cent", rc, 0), ("cent", rc, 1)], [("out", c, bh)], lambda e: nc.sync.dma_start(
-                out=out[bh * P : (bh + 1) * P, c, :], in_=cent[rc][:]))
-            i = ring("m", 2)
-            tp = m_ps[i][:].rearrange("p (g u m) -> p g u m", g=2, u=2)
-
-            def turn(e):
-                cw = cb[rb][:].bitcast(F32)
-                for gr in range(2):
-                    for u in range(2):
-                        nc.tensor.transpose(tp[:, gr, u, :], cw[:, 256 * gr + u : 256 * (gr + 1) : 2], ident[:])
-
-            task({"P": 550}, [("cb", rb)], [("m", i)], turn)
-
-            def planes_in(e):
-                copy_on(e, qc[bh][:, :, c, :].bitcast(F32).rearrange("p g (m u) -> p g m u", u=2), tp.rearrange("p g u m -> p g m u"))
-
-            task(either(440, 435, only), [("m", i)], [("qc", bh, c)], planes_in)
-
-        words_i = words.bitcast(I32).rearrange("g p m t -> p g (m t)")
-        scales_i = scales.bitcast(I32)
-        nat = sb("nat", [2, C * 4 * P], BF16)
-        p_codes = sb("p_codes", [2 * C * P], U32, 2)
-        p_scales = sb("p_scales", [2 * C * P], U8, 2)
-
-        def planes(bh):
-            m0 = bh * C * P
+        def finish(c, b_half, rounded, centred):
+            nc.sync.dma_start(out=out[b_half * P : (b_half + 1) * P, c, :], in_=centred[:])
+            pairs = take_turn()[:].rearrange("p (g u i) -> p g u i", g=2, u=2)
+            rows = rounded[:].bitcast(F32)
             for gr in range(2):
+                for u in range(2):
+                    nc.tensor.transpose(pairs[:, gr, u, :], rows[:, 256 * gr + u : 256 * (gr + 1) : 2], ident[:])
+            nc.scalar.copy(
+                out=for_planes[b_half][:, :, c, :].bitcast(F32).rearrange("p g (i u) -> p g i u", u=2),
+                in_=pairs.rearrange("p g u i -> p g i u"),
+            )
 
-                def mix(e, gr=gr):
-                    nc.vector.tensor_copy(
-                        out=nat[:, gr].rearrange("p (m c t) -> p m c t", c=C, t=4),
-                        in_=qc[bh][:, gr].rearrange("p c (m t) -> p m c t", t=4),
-                    )
+        words_out = words.bitcast(I32).rearrange("g p m t -> p g (m t)")
+        scales_out = scales.bitcast(I32)
+        half_cols = COORDS * P
 
-                task({"V": 330}, [("qc", bh, c) for c in range(C)], [("nat", gr)], mix)
-            flat = nat[:].rearrange("p g x -> p (g x)")
-            for lo, width in ((0, 512), (512, 256)):
-                task({"V": width}, [("nat", 0)] + ([("nat", 1)] if lo + width > C * P else []), [("pc", bh, lo)],
-                     quant(p_codes[bh][:, lo : lo + width], p_scales[bh][:, lo : lo + width], flat[:, 4 * lo : 4 * (lo + width)]))
-            keys = [("pc", bh, lo) for lo in (0, 512)]
-            task({"D": 700}, keys, [("words", bh)], lambda e: nc.sync.dma_start(
-                out=words_i[:, :, m0 : m0 + C * P], in_=p_codes[bh][:].rearrange("p (g m) -> p g m", g=2).bitcast(I32)))
+        by_column = kept("by_column", [2, PACK * half_cols], BF16)
+        take_codes = rotating("plane_codes", [2 * half_cols], U32, 2)
+        take_scales = rotating("plane_scales", [2 * half_cols], U8, 2)
+        calls = ((0, 512), (512, 256))
 
-            def store_scales(e):
-                for q in range(4):
-                    nc.sync.dma_start(
-                        out=scales_i[:, 4 * q : 4 * q + 4, bh * 96 : (bh + 1) * 96].rearrange("g r m -> r g m"),
-                        in_=p_scales[bh][32 * q : 32 * q + 4, :].bitcast(I32).rearrange("r (g m) -> r g m", g=2),
-                    )
+        def planes(b_half):
+            for gr in range(2):
+                nc.vector.tensor_copy(
+                    out=by_column[:, gr].rearrange("p (i c t) -> p i c t", c=COORDS, t=PACK),
+                    in_=for_planes[b_half][:, gr].rearrange("p c (i t) -> p i c t", t=PACK),
+                )
+            codes = take_codes()
+            scale_rows = take_scales()
+            values = by_column[:].rearrange("p g x -> p (g x)")
+            for first, n in calls:
+                span = slice(first, first + n)
+                quantize(codes[:, span], scale_rows[:, span], values[:, PACK * first : PACK * (first + n)])
+            m0 = b_half * half_cols
+            nc.sync.dma_start(
+                out=words_out[:, :, m0 : m0 + half_cols],
+                in_=codes[:].rearrange("p (g m) -> p g m", g=2).bitcast(I32),
+            )
+            for quadrant in range(4):
+                live = scale_rows[32 * quadrant : 32 * quadrant + 4, :].bitcast(I32)
+                rows_out = scales_out[:, 4 * quadrant : 4 * quadrant + 4, m0 // 4 : (m0 + half_cols) // 4]
+                nc.sync.dma_start(
+                    out=rows_out.rearrange("g r m -> r g m"), in_=live.rearrange("r (g m) -> r g m", g=2)
+                )
 
-            task({"D": 300}, keys, [("scales", bh)], store_scales)
-
-        makers = {"W": w_block, "Z": z_all, "V": coef, "S": s_piece, "B": stage1, "K": pack_u, "Q": pack_u_tensor, "C": m_tile, "M": mean_first, "R": planes}
-        for item in ORDER.split(","):
-            parts = item.split()
-            makers[parts[0]](*[int(x) if x in "0123456789" else x for x in parts[1:]])
-        for i, e in sorted([(i, e) for start, e, i in list_schedule(tasks)]):
-            costs, reads, writes, emit = tasks[i]
-            if emit is not None:
-                emit(e)
+        makers = {
+            "coefficients": coefficients,
+            "w": quantize_w,
+            "s": quantize_s,
+            "z": quantize_z,
+            "stage1": stage1,
+            "u": quantize_u,
+            "tile_tensor_mean": tile_tensor_mean,
+            "tile_scalar_mean": tile_scalar_mean,
+            "planes": planes,
+        }
+        for step in PLAN:
+            makers[step[0]](*step[1:])

from contextlib import ExitStack

import concourse.mybir as mybir
from concourse.masks import make_identity

F32 = mybir.dt.float32
BF16 = mybir.dt.bfloat16
U32 = mybir.dt.uint32
I32 = mybir.dt.int32
U8 = mybir.dt.uint8
FP8X4 = mybir.dt.float8_e4m3fn_x4
ACT = mybir.ActivationFunctionType
ALU = mybir.AluOpType

P = 128
PACK = 4
BATCH, LATENT, COORDS, FACES, VERTS = 256, 512, 3, 512, 1024
JAC = COORDS * COORDS * FACES
BANK = 512
EPS = 1e-6
FLOPS = 2 * BATCH * LATENT * JAC + 2 * BATCH * COORDS * COORDS * FACES * VERTS

LOADS = (
    ("w", 1, 1), ("vectors",), ("w", 2, 1), ("z",), ("s", 0), ("w", 0, 1), ("s", 1), ("w", 5, 1), ("w", 6, 1),
    ("w", 7, 2), ("s", 2), ("w", 3, 1), ("w", 4, 1),
)

PLAN = (
    ("coefficients",), ("w", 1, "V"), ("s", 0, "V"), ("z",), ("w", 2, "S"), ("w", 0, "VS"), ("s", 2, "V"),
    ("stage1", 0, 1), ("s", 1, "S"), ("w", 5, "VS"), ("s", 4, "S"), ("w", 7, "V"), ("w", 3, "S"),
    ("stage1", 0, 0), ("w", 6, "S"), ("w", 4, "S"), ("stage1", 1, 1), ("w", 8, "VS"), ("stage1", 1, 0),
    ("u", 0, "VVV"), ("s", 3, "V"), ("s", 5, "S"), ("u", 1, "VVV"), ("stage1", 2, 0), ("stage1", 2, 1),
    ("tile_tensor_mean", 0, 1), ("u", 2, "SSV"), ("tile_tensor_mean", 0, 0), ("tile_scalar_mean", 1, 0, "V"),
    ("tile_scalar_mean", 1, 1, "V"), ("tile_scalar_mean", 2, 0, "V"), ("planes", 0),
    ("tile_scalar_mean", 2, 1, "S"), ("planes", 1),
)


def tile_neuraljacobianfieldpoissonintegration_x1_kernel(tc, z, w, b, nrm, g, s, out, words, scales):
    nc = tc.nc
    with ExitStack() as ctx:
        sbuf = ctx.enter_context(tc.tile_pool(name="sbuf", bufs=1))
        psum = ctx.enter_context(tc.psum_pool(name="psum", bufs=1))

        def kept(name, shape, dtype):
            return sbuf.tile([P] + shape, dtype, name=name, align_bytes=64)

        def rotation(tiles):
            taken = []

            def take():
                taken.append(len(taken))
                return tiles[taken[-1] % len(tiles)]

            return take

        def rotating(name, shape, dtype, n):
            return rotation([kept("%s%d" % (name, i), shape, dtype) for i in range(n)])

        def banks(name, n):
            return rotation([psum.tile([P, BANK], F32, name="%s%d" % (name, i)) for i in range(n)])

        take_h, take_y, take_turn = banks("h", 4), banks("y", 2), banks("turn", 2)

        def copy_on(engine, dst, src):
            if engine == "S":
                nc.scalar.copy(out=dst, in_=src)
            else:
                nc.vector.tensor_copy(out=dst, in_=src)

        def quantize(codes, scale_rows, values):
            nc.vector.quantize_mx(out=codes.bitcast(FP8X4), scales=scale_rows, in_=values)

        vectors = kept("vectors", [FACES], BF16)
        nc.vector.memset(vectors[:], 0.0)
        ident_bf = kept("ident_bf", [P], BF16)
        ident = kept("ident", [P], F32)
        make_identity(nc, ident_bf[:])
        make_identity(nc, ident[:])

        w_block_raw = {}
        s_raw = {}
        z_raw = kept("z_raw", [2, LATENT], BF16)

        def load_w(first, n):
            raw = kept("w_raw%d" % first, [PACK, n * FACES], BF16)
            cols = w[:, first * FACES : (first + n) * FACES]
            nc.sync.dma_start(out=raw[:], in_=cols.rearrange("(p t) j -> p t j", t=PACK))
            for i in range(n):
                w_block_raw[first + i] = raw[:, :, i * FACES : (i + 1) * FACES]

        def load_s(k):
            s_raw[k] = kept("s_raw%d" % k, [PACK, VERTS], BF16)
            rows = s[k * FACES : (k + 1) * FACES, :]
            nc.sync.dma_start(out=s_raw[k][:], in_=rows.rearrange("(p t) v -> p t v", t=PACK))

        def load_z():
            nc.sync.dma_start(out=z_raw[:], in_=z.rearrange("(r p) d -> p r d", p=P))

        def load_vectors():
            nc.sync.dma_start(out=vectors[0:3, :], in_=nrm)
            nc.sync.dma_start(out=vectors[3:6, :], in_=g)
            nc.sync.dma_start(out=vectors[6:15, :], in_=b.rearrange("(r f) -> r f", f=FACES))

        loaders = {"w": load_w, "s": load_s, "z": load_z, "vectors": load_vectors}
        for load in LOADS:
            loaders[load[0]](*load[1:])

        face = kept("face", [15, PACK], F32)
        normal_in, gain = face[:, 0:3, :], face[:, 3:6, :]
        minus_half = kept("minus_half", [PACK], F32)
        nc.gpsimd.memset(minus_half[:], -0.5)
        normal = kept("normal", [COORDS, PACK], F32)
        minus_gn = kept("minus_gn", [COORDS, PACK], F32)
        gain_bias = kept("gain_bias", [COORDS, COORDS, PACK], F32)
        normal_bias = kept("normal_bias", [COORDS, PACK], F32)

        def coefficients():
            turned_vectors = take_turn()[:].bitcast(BF16)
            for t in range(PACK):
                nc.tensor.transpose(turned_vectors[:, t * P : (t + 1) * P], vectors[:, t:FACES:PACK], ident_bf[:])
            by_t = turned_vectors[:, 0 : PACK * P].rearrange("p (t r) -> p t r", t=PACK)
            nc.vector.tensor_copy(out=face[:], in_=by_t[:, :, 0:15].rearrange("p t r -> p r t"))

            def combine(dst, in0, in1, op):
                nc.gpsimd.tensor_tensor(out=dst, in0=in0, in1=in1, op=op)

            square = kept("square", [COORDS, PACK], F32)
            two = kept("two", [PACK], F32)
            three = kept("three", [PACK], F32)
            shifted = kept("shifted", [PACK], F32)
            inverse = kept("inverse", [PACK], F32)
            gn = kept("gn", [COORDS, PACK], F32)
            nb = kept("nb", [COORDS, COORDS, PACK], F32)
            nb_two = kept("nb_two", [COORDS, PACK], F32)

            combine(square[:], normal_in, normal_in, ALU.mult)
            combine(two[:], square[:, 0, :], square[:, 1, :], ALU.add)
            combine(three[:], two[:], square[:, 2, :], ALU.add)
            nc.gpsimd.tensor_scalar(
                out=shifted[:], in0=three[:], scalar1=EPS, scalar2=1.0, op0=ALU.add, op1=ALU.mult
            )
            combine(inverse[:], shifted[:], minus_half[:], ALU.pow)
            combine(normal[:], normal_in, inverse[:].unsqueeze(1).to_broadcast([P, COORDS, PACK]), ALU.mult)
            combine(gn[:], normal[:], gain, ALU.mult)
            nc.gpsimd.tensor_scalar(
                out=minus_gn[:], in0=gn[:], scalar1=0.0, scalar2=-1.0, op0=ALU.add, op1=ALU.mult
            )
            bias = face[:, 6:15, :].rearrange("p (c k) t -> p c (k t)", c=COORDS)

            def for_each_c(per_k):
                return per_k.rearrange("p k t -> p (k t)").unsqueeze(1).to_broadcast([P, COORDS, COORDS * PACK])

            combine(gain_bias[:].rearrange("p c k t -> p c (k t)"), bias, for_each_c(gain), ALU.mult)
            combine(nb[:].rearrange("p c k t -> p c (k t)"), bias, for_each_c(normal[:]), ALU.mult)
            combine(nb_two[:], nb[:, :, 0, :], nb[:, :, 1, :], ALU.add)
            combine(normal_bias[:], nb_two[:], nb[:, :, 2, :], ALU.add)

        w_codes = kept("w_codes", [JAC], U32)
        w_scales = kept("w_scales", [JAC], U8)

        take_grouped = rotating("grouped", [PACK * FACES], BF16, 5)

        def quantize_w(block, engines):
            grouped = take_grouped()
            dst = grouped[:].rearrange("p (t m j) -> p m t j", t=PACK, j=PACK)
            src = w_block_raw[block].rearrange("p j (m t) -> p m t j", t=PACK)
            share = P // len(engines)
            for i, engine in enumerate(engines):
                part = slice(i * share, (i + 1) * share)
                copy_on(engine, dst[:, part], src[:, part])
            cols = slice(block * FACES, (block + 1) * FACES)
            quantize(w_codes[:, cols], w_scales[:, cols], grouped[:])

        z_codes = kept("z_codes", [BATCH], U32)
        z_scales = kept("z_scales", [BATCH], U8)

        def quantize_z():
            pairs = take_turn()[:].rearrange("p (u i) -> p u i", u=2)
            for r in range(2):
                rows = z_raw[:, r, :].bitcast(F32)
                for u in range(2):
                    nc.tensor.transpose(pairs[:, u, r * P : (r + 1) * P], rows[:, u : LATENT // 2 : 2], ident[:])
            grouped = kept("z_grouped", [PACK * BATCH], BF16)
            nc.vector.tensor_copy(
                out=grouped[:].bitcast(F32).rearrange("p (i u) -> p i u", u=2), in_=pairs.rearrange("p u i -> p i u")
            )
            quantize(z_codes[:], z_scales[:], grouped[:])

        s_codes = kept("s_codes", [COORDS * VERTS], U32)
        s_scales = kept("s_scales", [COORDS * VERTS], U8)

        def interleave(engine, dst, src):
            copy_on(
                engine, dst.rearrange("p (x i t) -> p x t i", i=4, t=PACK), src.rearrange("p t (x i) -> p x t i", i=4)
            )

        def quantize_s(half, engine):
            k, v_half = divmod(half, 2)
            grouped = take_grouped()
            interleave(engine, grouped[:], s_raw[k][:, :, v_half * BANK : (v_half + 1) * BANK])
            cols = slice(half * BANK, (half + 1) * BANK)
            quantize(s_codes[:, cols], s_scales[:, cols], grouped[:])

        u_first = [kept("u_first%d" % k, [PACK, 2 * BATCH], BF16) for k in range(COORDS)]
        u_last = [kept("u_last%d" % k, [PACK, BATCH], BF16) for k in range(COORDS)]

        def u_of(c, k):
            return u_last[k][:] if c == 2 else u_first[k][:, :, c * BATCH : (c + 1) * BATCH]

        take_along0 = rotating("along0_", [2 * BATCH], F32, 2)
        take_along01 = rotating("along01_", [2 * BATCH], F32, 2)
        take_along = rotating("along", [2 * BATCH], F32, 2)
        take_scaled = rotating("scaled", [2 * BATCH], F32, 6)

        def halves(tile):
            return [tile[:, i * BATCH : (i + 1) * BATCH] for i in range(2)]

        def stage1(c, pair):
            slices = (2 * pair, 2 * pair + 1)
            h = []
            for k in range(COORDS):
                h_k = take_h()
                for i, t in enumerate(slices):
                    col = (c * COORDS + k) * FACES + t * P
                    nc.tensor.matmul_mx(
                        out=h_k[:, i * BATCH : (i + 1) * BATCH],
                        lhsT=w_codes[:, col : col + P].bitcast(FP8X4),
                        lhsT_scale=w_scales[:, col : col + P],
                        rhs=z_codes[:].bitcast(FP8X4),
                        rhs_scale=z_scales[:],
                        start=True,
                        stop=True,
                    )
                h.append(halves(h_k))

            along0, along01, along = halves(take_along0()), halves(take_along01()), halves(take_along())
            scaled = [halves(take_scaled()) for k in range(COORDS)]

            def scale_h(k):
                for i, t in enumerate(slices):
                    nc.scalar.activation(
                        out=scaled[k][i], in_=h[k][i], func=ACT.Identity,
                        scale=face[:, 3 + k, t : t + 1], bias=gain_bias[:, c, k, t : t + 1],
                    )

            def multiply_add(dst, in0, per_face, in1):
                nc.vector.scalar_tensor_tensor(
                    out=dst, in0=in0, scalar=per_face, in1=in1, op0=ALU.mult, op1=ALU.add
                )

            scale_h(1)
            for i, t in enumerate(slices):
                nc.scalar.activation(
                    out=along0[i], in_=h[0][i], func=ACT.Identity,
                    scale=normal[:, 0, t : t + 1], bias=normal_bias[:, c, t : t + 1],
                )
            scale_h(2)
            for i, t in enumerate(slices):
                multiply_add(along01[i], h[1][i], normal[:, 1, t : t + 1], along0[i])
            for i, t in enumerate(slices):
                multiply_add(along[i], h[2][i], normal[:, 2, t : t + 1], along01[i])
            scale_h(0)
            for k in (1, 2, 0):
                for i, t in enumerate(slices):
                    multiply_add(u_of(c, k)[:, t, :], along[i], minus_gn[:, k, t : t + 1], scaled[k][i])

        u_codes = [kept("u_codes%d" % c, [COORDS * BATCH], U32) for c in range(COORDS)]
        u_scales = [kept("u_scales%d" % c, [COORDS * BATCH], U8) for c in range(COORDS)]

        take_u_grouped = rotating("u_grouped", [PACK * BATCH], BF16, 3)

        def quantize_u(c, engines):
            for k in range(COORDS):
                grouped = take_u_grouped()
                interleave(engines[k], grouped[:], u_of(c, k))
                cols = slice(k * BATCH, (k + 1) * BATCH)
                quantize(u_codes[c][:, cols], u_scales[c][:, cols], grouped[:])

        for_planes = [kept("for_planes%d" % b_half, [2, COORDS, PACK * P], BF16) for b_half in range(2)]

        take_rounded = rotating("rounded", [VERTS], BF16, 3)
        take_centred = rotating("centred", [VERTS], F32, 2)
        take_raw = rotating("raw", [VERTS], F32, 2)
        take_sums = rotating("sums", [2], F32, 2)
        take_minus_mean = rotating("minus_mean", [1], F32, 2)
        take_written = rotating("written", [P], BF16, 2)

        def pass_over(dst, c, b_half, k, v, n, start, stop):
            row = k * BATCH + b_half * P
            col = k * VERTS + v
            nc.tensor.matmul_mx(
                out=dst,
                lhsT=u_codes[c][:, row : row + P].bitcast(FP8X4),
                lhsT_scale=u_scales[c][:, row : row + P],
                rhs=s_codes[:, col : col + n].bitcast(FP8X4),
                rhs_scale=s_scales[:, col : col + n],
                start=start,
                stop=stop,
            )

        def product(c, b_half, v_half):
            y = take_y()
            for k in range(COORDS):
                pass_over(y[:], c, b_half, k, v_half * BANK, BANK, k == 0, k == COORDS - 1)
            return y

        def tile_tensor_mean(c, b_half):
            rounded = take_rounded()
            centred = take_centred()
            minus_mean = take_minus_mean()
            folded = take_turn()
            for k in range(COORDS):
                for v in range(0, VERTS, P):
                    pass_over(
                        folded[:, 0:P], c, b_half, k, v, P,
                        k == 0 and v == 0, k == COORDS - 1 and v == VERTS - P,
                    )
            written = take_written()
            nc.scalar.activation(
                out=written[:], in_=folded[:, 0:P], func=ACT.Identity, scale=-1.0 / VERTS, accum_out=minus_mean[:]
            )
            for v_half in range(2):
                y = product(c, b_half, v_half)
                nc.scalar.activation(
                    out=centred[:, v_half * BANK : (v_half + 1) * BANK], in_=y[:], func=ACT.Identity, bias=minus_mean[:]
                )
            nc.scalar.copy(out=rounded[:], in_=centred[:])
            finish(c, b_half, rounded, centred)

        def tile_scalar_mean(c, b_half, engine):
            raw = take_raw()
            rounded = take_rounded()
            centred = take_centred()
            sums = take_sums()
            minus_mean = take_minus_mean()
            for v_half in range(2):
                y = product(c, b_half, v_half)
                nc.scalar.activation(
                    out=raw[:, v_half * BANK : (v_half + 1) * BANK], in_=y[:], func=ACT.Identity,
                    accum_out=sums[:, v_half : v_half + 1],
                )
            nc.vector.tensor_scalar(
                out=minus_mean[:], in0=sums[:, 0:1], scalar1=sums[:, 1:2], scalar2=-1.0 / VERTS,
                op0=ALU.add, op1=ALU.mult,
            )
            nc.vector.tensor_scalar(out=rounded[:], in0=raw[:], scalar1=minus_mean[:], scalar2=None, op0=ALU.add)
            if engine == "S":
                nc.scalar.activation(out=centred[:], in_=raw[:], func=ACT.Identity, bias=minus_mean[:])
            else:
                nc.vector.tensor_scalar(out=centred[:], in0=raw[:], scalar1=minus_mean[:], scalar2=None, op0=ALU.add)
            finish(c, b_half, rounded, centred)

        def finish(c, b_half, rounded, centred):
            nc.sync.dma_start(out=out[b_half * P : (b_half + 1) * P, c, :], in_=centred[:])
            pairs = take_turn()[:].rearrange("p (g u i) -> p g u i", g=2, u=2)
            rows = rounded[:].bitcast(F32)
            for gr in range(2):
                for u in range(2):
                    nc.tensor.transpose(pairs[:, gr, u, :], rows[:, 256 * gr + u : 256 * (gr + 1) : 2], ident[:])
            nc.scalar.copy(
                out=for_planes[b_half][:, :, c, :].bitcast(F32).rearrange("p g (i u) -> p g i u", u=2),
                in_=pairs.rearrange("p g u i -> p g i u"),
            )

        words_out = words.bitcast(I32).rearrange("g p m t -> p g (m t)")
        scales_out = scales.bitcast(I32)
        half_cols = COORDS * P

        by_column = kept("by_column", [2, PACK * half_cols], BF16)
        take_codes = rotating("plane_codes", [2 * half_cols], U32, 2)
        take_scales = rotating("plane_scales", [2 * half_cols], U8, 2)
        calls = ((0, 512), (512, 256))

        def planes(b_half):
            for gr in range(2):
                nc.vector.tensor_copy(
                    out=by_column[:, gr].rearrange("p (i c t) -> p i c t", c=COORDS, t=PACK),
                    in_=for_planes[b_half][:, gr].rearrange("p c (i t) -> p i c t", t=PACK),
                )
            codes = take_codes()
            scale_rows = take_scales()
            values = by_column[:].rearrange("p g x -> p (g x)")
            for first, n in calls:
                span = slice(first, first + n)
                quantize(codes[:, span], scale_rows[:, span], values[:, PACK * first : PACK * (first + n)])
            m0 = b_half * half_cols
            nc.sync.dma_start(
                out=words_out[:, :, m0 : m0 + half_cols],
                in_=codes[:].rearrange("p (g m) -> p g m", g=2).bitcast(I32),
            )
            for quadrant in range(4):
                live = scale_rows[32 * quadrant : 32 * quadrant + 4, :].bitcast(I32)
                rows_out = scales_out[:, 4 * quadrant : 4 * quadrant + 4, m0 // 4 : (m0 + half_cols) // 4]
                nc.sync.dma_start(
                    out=rows_out.rearrange("g r m -> r g m"), in_=live.rearrange("r (g m) -> r g m", g=2)
                )

        makers = {
            "coefficients": coefficients,
            "w": quantize_w,
            "s": quantize_s,
            "z": quantize_z,
            "stage1": stage1,
            "u": quantize_u,
            "tile_tensor_mean": tile_tensor_mean,
            "tile_scalar_mean": tile_scalar_mean,
            "planes": planes,
        }
        for step in PLAN:
            makers[step[0]](*step[1:])
